import numpy as np
import ml_dtypes


def mxq(x, axis, fmt="e4m3"):
    dtype, down = {"e4m3": (ml_dtypes.float8_e4m3fn, 7), "e5m2": (ml_dtypes.float8_e5m2, 14)}[fmt]
    v = np.moveaxis(np.asarray(x, np.float32).astype(ml_dtypes.bfloat16).astype(np.float64), axis, -1)
    blocks = v.reshape(v.shape[:-1] + (-1, 32))
    amax = np.abs(blocks).max(-1, keepdims=True)
    byte = np.maximum(np.where(amax > 0, np.frexp(amax)[1] - 1 + 127, 0) - down, 1)
    scale = np.exp2(byte - 127.0)
    codes = (blocks / scale).astype(np.float32).astype(dtype).astype(np.float64)
    return np.moveaxis((codes * scale).reshape(v.shape), -1, axis)


WIDE = False


def mx_kscale(k):
    if not WIDE:
        return np.ones(k)
    levels = np.array([10, -10, 5, -5, 0])
    if k % 512:
        return np.exp2(np.random.permutation(np.resize(levels, k // 32))).repeat(32)
    a = np.empty((k // 512, 16))
    for p in range(k // 512):
        a[p, :8] = np.random.permutation(np.resize(levels, 8))
        for g in range(8):
            far = levels[np.abs(levels - a[p, g]) >= 10]
            a[p, g + 8] = far[np.random.randint(len(far))]
    return np.exp2(a.ravel()).repeat(32)


def f64(x):
    return np.asarray(x).astype(np.float64)


def striped(idx):
    return np.tile(idx.reshape(-1, 16).T, (8, 1)).astype(np.uint16)


def unstriped(offs):
    return offs[:16].T.reshape(-1).astype(np.int64)


def pack_weight(w):
    k, n = w.shape
    w = f64(np.asarray(w, np.float32).astype(ml_dtypes.bfloat16)).reshape(k // 32, 32, n)
    amax = np.abs(w).max(1)
    byte = np.clip(np.where(amax > 0, np.frexp(amax)[1] - 1 + 127 - 7, 1), 1, 254)
    scaled = (w * np.exp2(127.0 - byte)[:, None, :]).reshape(k, n).astype(np.float32)
    words = np.ascontiguousarray(scaled.reshape(k // 512, 128, 4, n).transpose(0, 1, 3, 2)).astype(ml_dtypes.float8_e4m3fn).view(np.uint8)
    return words, np.ascontiguousarray(byte.astype(np.uint8).reshape(k // 512, 16, n))


def unpack_weight(words, scales):
    g, p, n, _ = words.shape
    vals = np.ascontiguousarray(words).view(ml_dtypes.float8_e4m3fn).astype(np.float64) * np.repeat(np.exp2(scales.astype(np.float64) - 127.0), 8, axis=1)[..., None]
    return vals.transpose(0, 1, 3, 2).reshape(g * 512, n)


K, T, E, C, N = 2048, 1024, 8, 128, 128


def by_expert(wq, xq):
    return np.concatenate([wq[e].T @ xq[:, e * C:(e + 1) * C] for e in range(E)], axis=1)


def setup_inputs():
    n = np.random.standard_normal
    s = mx_kscale(K)[:, None]
    packed = [pack_weight(m) for m in n((E, K, N)) / np.sqrt(K) / s[None]]
    return {
        "xT": (n((K, T)) * s).astype(np.float32),
        "w_words": np.stack([m[0] for m in packed]),
        "w_scales": np.stack([m[1] for m in packed]),
        "gate": np.tile(np.random.uniform(0.2, 1.0, E * C), (N, 1)).astype(np.float32),
        "offs": striped(np.random.permutation(T)[:E * C]),
    }


def reference(xT, w_words, w_scales, gate, offs):
    idx = unstriped(offs)
    xq = mxq(f64(xT)[:, idx], 0, "e4m3")
    w = np.stack([unpack_weight(w_words[e], w_scales[e]) for e in range(E)])
    y = by_expert(w, xq)
    out = np.zeros((N, T))
    out[:, idx] = f64(gate) * y
    return out

@@ -1,0 +1,144 @@
+from contextlib import ExitStack
+
+import concourse.mybir as mybir
+
+K, T, E, C, N = 2048, 1024, 8, 128, 128
+FLOPS = 2 * K * N * E * C
+
+F32 = mybir.dt.float32
+BF16 = mybir.dt.bfloat16
+U32 = mybir.dt.uint32
+I32 = mybir.dt.int32
+U16 = mybir.dt.uint16
+U8 = mybir.dt.uint8
+FP8X4 = mybir.dt.float8_e4m3fn_x4
+MULT = mybir.AluOpType.mult
+
+P = 128
+PACK = 4
+PASSES = K // (P * PACK)
+HALF = 512
+HALVES = (E * C) // HALF
+EXPERTS_A_HALF = HALF // C
+PIECE = 256
+
+
+def tile_routed_moe_kernel(tc, xT, w_words, w_scales, gate, offs, out):
+    nc = tc.nc
+    with ExitStack() as ctx:
+        keep = ctx.enter_context(tc.tile_pool(name="keep", bufs=1))
+        ring = ctx.enter_context(tc.tile_pool(name="ring", bufs=3))
+        psum = ctx.enter_context(tc.psum_pool(name="psum", bufs=1))
+
+        offsets = keep.tile([P, (E * C) // 16], U16, name="offsets")
+        nc.sync.dma_start(offsets[:], offs)
+
+        w_planes = keep.tile([P, E * PASSES, N], U8, name="w_planes", align_bytes=64)
+        nc.vector.memset(w_planes[:].rearrange("p g n -> p (g n)").bitcast(I32), 0)
+
+        x_view = xT.rearrange("(g p t) n -> g p t n", p=P, t=PACK)
+        planes = {}
+
+        def load_pass(g):
+            for t in range(PACK):
+                plane = keep.tile([P, T], F32, name="plane%d_%d" % (g, t))
+                nc.sync.dma_start(plane[:], x_view[g, :, t, :])
+                planes[(g, t)] = plane
+
+        load_pass(0)
+        load_pass(1)
+        s_view = w_scales.rearrange("e a (q i) n -> i q (e a) n", i=4)
+        for i in range(4):
+            nc.sync.dma_start(w_planes[i:P:32, :, :].bitcast(I32), s_view[i].bitcast(I32))
+        w_codes = []
+        for a in range(PASSES):
+            wq = keep.tile([P, E, N], U32, name="w_codes%d" % a, align_bytes=64)
+            nc.sync.dma_start(wq[:].bitcast(I32), w_words[:, a].rearrange("e p n r -> p e (n r)").bitcast(I32))
+            w_codes.append(wq)
+        load_pass(2)
+        load_pass(3)
+        gate_sb = keep.tile([P, E * C], F32, name="gate_sb")
+        nc.sync.dma_start(gate_sb[:], gate)
+
+        acc = [psum.tile([N, C], F32, name="acc%d" % e) for e in range(E)]
+        sums = [keep.tile([N, HALF], F32, name="sums%d" % h) for h in range(HALVES)]
+        window = keep.tile([N, T], F32, name="window")
+
+        units = [(g, h) for g in range(PASSES) for h in range(HALVES)]
+        gathered = {}
+        grouped = {}
+
+        def gather(u, ts):
+            g, h = u
+            if u not in gathered:
+                g4 = ring.tile([P, PACK, HALF], F32, name="g4")
+                gathered[u] = g4
+            for t in ts:
+                nc.vector.tensor_copy(
+                    gathered[u][:, t, :],
+                    planes[(g, t)][:].indirect(offsets[:, h * (HALF // 16) : (h + 1) * (HALF // 16)]),
+                )
+
+        def interleave(u, parts):
+            gr = ring.tile([P, HALF, PACK], BF16, name="gr", align_bytes=64)
+            grouped[u] = gr
+            width = HALF // parts
+            for s in range(parts):
+                cols = slice(s * width, (s + 1) * width)
+                nc.scalar.copy(gr[:, cols, :], gathered[u][:, :, cols].rearrange("p t c -> p c t"))
+
+        def quantise_and_multiply(u, parts, s):
+            g, h = u
+            width = HALF // parts
+            codes = keep.tile([P, width], U32, name="codes%d_%d_%d" % (g, h, s), align_bytes=64)
+            scales = keep.tile([P, width], U8, name="scales%d_%d_%d" % (g, h, s), align_bytes=64)
+            nc.vector.quantize_mx(
+                out=codes[:].bitcast(FP8X4),
+                scales=scales[:],
+                in_=grouped[u][:, s * width : (s + 1) * width, :].rearrange("p c t -> p (c t)"),
+            )
+            for j in range(width // C):
+                e = h * EXPERTS_A_HALF + s * (width // C) + j
+                nc.tensor.matmul_mx(
+                    out=acc[e][:],
+                    lhsT=w_codes[g][:, e, :].bitcast(FP8X4),
+                    lhsT_scale=w_planes[:, e * PASSES + g, :],
+                    rhs=codes[:, j * C : (j + 1) * C].bitcast(FP8X4),
+                    rhs_scale=scales[:, j * C : (j + 1) * C],
+                    start=(g == 0),
+                    stop=(g == PASSES - 1),
+                )
+
+        def empty_banks(h, js):
+            for j in js:
+                nc.scalar.copy(sums[h][:, j * C : (j + 1) * C], acc[h * EXPERTS_A_HALF + j][:])
+
+        def scatter(h, s):
+            first = h * HALF + s * PIECE
+            nc.vector.tensor_tensor(
+                window[:].indirect(offsets[:, first // 16 : (first + PIECE) // 16]),
+                sums[h][:, s * PIECE : (s + 1) * PIECE],
+                gate_sb[:, first : first + PIECE],
+                MULT,
+            )
+
+        last = len(units) - 1
+        for i in range(last):
+            gather(units[i], range(PACK))
+            if i > 0:
+                quantise_and_multiply(units[i - 1], 1, 0)
+            interleave(units[i], 1)
+        gather(units[last], (0, 1))
+        quantise_and_multiply(units[last - 1], 1, 0)
+        empty_banks(0, range(EXPERTS_A_HALF))
+        gather(units[last], (2, 3))
+        interleave(units[last], 2)
+        scatter(0, 0)
+        quantise_and_multiply(units[last], 2, 0)
+        empty_banks(1, (0, 1))
+        scatter(0, 1)
+        quantise_and_multiply(units[last], 2, 1)
+        empty_banks(1, (2, 3))
+        scatter(1, 0)
+        scatter(1, 1)
+        nc.sync.dma_start(out, window[:])

@@ -13,13 +13,11 @@ U16 = mybir.dt.uint16
 U8 = mybir.dt.uint8
 FP8X4 = mybir.dt.float8_e4m3fn_x4
 MULT = mybir.AluOpType.mult
+COPY = mybir.ActivationFunctionType.Copy
 
 P = 128
 PACK = 4
 PASSES = K // (P * PACK)
-HALF = 512
-HALVES = (E * C) // HALF
-EXPERTS_A_HALF = HALF // C
 PIECE = 256
 
 
@@ -27,7 +25,6 @@ def tile_routed_moe_kernel(tc, xT, w_words, w_scales, gate, offs, out):
     nc = tc.nc
     with ExitStack() as ctx:
         keep = ctx.enter_context(tc.tile_pool(name="keep", bufs=1))
-        ring = ctx.enter_context(tc.tile_pool(name="ring", bufs=3))
         psum = ctx.enter_context(tc.psum_pool(name="psum", bufs=1))
 
         offsets = keep.tile([P, (E * C) // 16], U16, name="offsets")
@@ -37,16 +34,18 @@ def tile_routed_moe_kernel(tc, xT, w_words, w_scales, gate, offs, out):
         nc.vector.memset(w_planes[:].rearrange("p g n -> p (g n)").bitcast(I32), 0)
 
         x_view = xT.rearrange("(g p t) n -> g p t n", p=P, t=PACK)
-        planes = {}
+        raw = [keep.tile([P, PACK, T], F32, name="raw%d" % g) for g in range(PASSES)]
+        rounded = {g: keep.tile([P, PACK, T], BF16, name="rounded%d" % g) for g in (1, 3)}
 
-        def load_pass(g):
+        def load(g, t):
+            nc.sync.dma_start(raw[g][:, t, :], x_view[g, :, t, :])
+
+        for t in range(PACK):
+            load(0, t)
+            load(1, t)
+        for g in (3, 2):
             for t in range(PACK):
-                plane = keep.tile([P, T], F32, name="plane%d_%d" % (g, t))
-                nc.sync.dma_start(plane[:], x_view[g, :, t, :])
-                planes[(g, t)] = plane
-
-        load_pass(0)
-        load_pass(1)
+                load(g, t)
         s_view = w_scales.rearrange("e a (q i) n -> i q (e a) n", i=4)
         for i in range(4):
             nc.sync.dma_start(w_planes[i:P:32, :, :].bitcast(I32), s_view[i].bitcast(I32))
@@ -55,50 +54,43 @@ def tile_routed_moe_kernel(tc, xT, w_words, w_scales, gate, offs, out):
             wq = keep.tile([P, E, N], U32, name="w_codes%d" % a, align_bytes=64)
             nc.sync.dma_start(wq[:].bitcast(I32), w_words[:, a].rearrange("e p n r -> p e (n r)").bitcast(I32))
             w_codes.append(wq)
-        load_pass(2)
-        load_pass(3)
         gate_sb = keep.tile([P, E * C], F32, name="gate_sb")
         nc.sync.dma_start(gate_sb[:], gate)
 
         acc = [psum.tile([N, C], F32, name="acc%d" % e) for e in range(E)]
-        sums = [keep.tile([N, HALF], F32, name="sums%d" % h) for h in range(HALVES)]
+        sums = [keep.tile([N, PIECE], F32, name="sums%d" % s) for s in range((E * C) // PIECE)]
         window = keep.tile([N, T], F32, name="window")
 
-        units = [(g, h) for g in range(PASSES) for h in range(HALVES)]
-        gathered = {}
         grouped = {}
 
-        def gather(u, ts):
-            g, h = u
-            if u not in gathered:
-                g4 = ring.tile([P, PACK, HALF], F32, name="g4")
-                gathered[u] = g4
-            for t in ts:
-                nc.vector.tensor_copy(
-                    gathered[u][:, t, :],
-                    planes[(g, t)][:].indirect(offsets[:, h * (HALF // 16) : (h + 1) * (HALF // 16)]),
-                )
+        def target(g, first, width, t):
+            if (g, first) not in grouped:
+                grouped[(g, first)] = keep.tile([P, width, PACK], BF16, name="grouped%d_%d" % (g, first), align_bytes=64)
+            return grouped[(g, first)][:, :, t]
 
-        def interleave(u, parts):
-            gr = ring.tile([P, HALF, PACK], BF16, name="gr", align_bytes=64)
-            grouped[u] = gr
-            width = HALF // parts
-            for s in range(parts):
-                cols = slice(s * width, (s + 1) * width)
-                nc.scalar.copy(gr[:, cols, :], gathered[u][:, :, cols].rearrange("p t c -> p c t"))
+        def vector_gather(g, first, width, t):
+            nc.vector.tensor_copy(
+                target(g, first, width, t),
+                raw[g][:, t, :].indirect(offsets[:, first // 16 : (first + width) // 16]),
+            )
 
-        def quantise_and_multiply(u, parts, s):
-            g, h = u
-            width = HALF // parts
-            codes = keep.tile([P, width], U32, name="codes%d_%d_%d" % (g, h, s), align_bytes=64)
-            scales = keep.tile([P, width], U8, name="scales%d_%d_%d" % (g, h, s), align_bytes=64)
+        def scalar_gather(g, first, width, t):
+            nc.scalar.activation(
+                target(g, first, width, t),
+                rounded[g][:, t, :].indirect(offsets[:, first // 16 : (first + width) // 16]),
+                COPY,
+            )
+
+        def quantise_and_multiply(g, first, width):
+            codes = keep.tile([P, width], U32, name="codes%d_%d" % (g, first), align_bytes=64)
+            scales = keep.tile([P, width], U8, name="scales%d_%d" % (g, first), align_bytes=64)
             nc.vector.quantize_mx(
                 out=codes[:].bitcast(FP8X4),
                 scales=scales[:],
-                in_=grouped[u][:, s * width : (s + 1) * width, :].rearrange("p c t -> p (c t)"),
+                in_=grouped[(g, first)][:].rearrange("p c t -> p (c t)"),
             )
             for j in range(width // C):
-                e = h * EXPERTS_A_HALF + s * (width // C) + j
+                e = first // C + j
                 nc.tensor.matmul_mx(
                     out=acc[e][:],
                     lhsT=w_codes[g][:, e, :].bitcast(FP8X4),
@@ -109,36 +101,54 @@ def tile_routed_moe_kernel(tc, xT, w_words, w_scales, gate, offs, out):
                     stop=(g == PASSES - 1),
                 )
 
-        def empty_banks(h, js):
-            for j in js:
-                nc.scalar.copy(sums[h][:, j * C : (j + 1) * C], acc[h * EXPERTS_A_HALF + j][:])
+        def way_back_copy(s):
+            for j in range(PIECE // C):
+                nc.scalar.copy(sums[s][:, j * C : (j + 1) * C], acc[s * (PIECE // C) + j][:])
 
-        def scatter(h, s):
-            first = h * HALF + s * PIECE
+        def scatter(s):
+            first = s * PIECE
             nc.vector.tensor_tensor(
                 window[:].indirect(offsets[:, first // 16 : (first + PIECE) // 16]),
-                sums[h][:, s * PIECE : (s + 1) * PIECE],
+                sums[s][:],
                 gate_sb[:, first : first + PIECE],
                 MULT,
             )
 
-        last = len(units) - 1
-        for i in range(last):
-            gather(units[i], range(PACK))
-            if i > 0:
-                quantise_and_multiply(units[i - 1], 1, 0)
-            interleave(units[i], 1)
-        gather(units[last], (0, 1))
-        quantise_and_multiply(units[last - 1], 1, 0)
-        empty_banks(0, range(EXPERTS_A_HALF))
-        gather(units[last], (2, 3))
-        interleave(units[last], 2)
-        scatter(0, 0)
-        quantise_and_multiply(units[last], 2, 0)
-        empty_banks(1, (0, 1))
-        scatter(0, 1)
-        quantise_and_multiply(units[last], 2, 1)
-        empty_banks(1, (2, 3))
-        scatter(1, 0)
-        scatter(1, 1)
+        for t in range(PACK):
+            vector_gather(0, 0, 512, t)
+            vector_gather(0, 512, 512, t)
+            nc.scalar.copy(rounded[1][:, t, :], raw[1][:, t, :])
+            scalar_gather(1, 0, 512, t)
+            scalar_gather(1, 512, 512, t)
+        nc.vector.tensor_copy(rounded[3][:, 0, :], raw[3][:, 0, :])
+        quantise_and_multiply(0, 0, 512)
+        nc.vector.tensor_copy(rounded[3][:, 1, :], raw[3][:, 1, :])
+        quantise_and_multiply(0, 512, 512)
+        nc.vector.tensor_copy(rounded[3][:, 2, :], raw[3][:, 2, :])
+        nc.vector.tensor_copy(rounded[3][:, 3, :], raw[3][:, 3, :])
+        for t in range(PACK):
+            vector_gather(2, 0, 512, t)
+            scalar_gather(3, 0, 512, t)
+        quantise_and_multiply(1, 0, 512)
+        quantise_and_multiply(1, 512, 512)
+        vector_gather(2, 512, 512, 0)
+        quantise_and_multiply(2, 0, 512)
+        for t in range(1, PACK):
+            vector_gather(2, 512, 512, t)
+        for t in range(PACK):
+            scalar_gather(3, 512, 256, t)
+        quantise_and_multiply(3, 0, 512)
+        way_back_copy(0)
+        way_back_copy(1)
+        quantise_and_multiply(2, 512, 512)
+        scatter(0)
+        for t in range(PACK):
+            scalar_gather(3, 768, 256, t)
+        scatter(1)
+        quantise_and_multiply(3, 512, 256)
+        way_back_copy(2)
+        quantise_and_multiply(3, 768, 256)
+        way_back_copy(3)
+        scatter(2)
+        scatter(3)
         nc.sync.dma_start(out, window[:])

@@ -18,6 +18,8 @@ COPY = mybir.ActivationFunctionType.Copy
 P = 128
 PACK = 4
 PASSES = K // (P * PACK)
+SLOTS = E * C
+HALF = 512
 PIECE = 256
 
 
@@ -27,7 +29,7 @@ def tile_routed_moe_kernel(tc, xT, w_words, w_scales, gate, offs, out):
         keep = ctx.enter_context(tc.tile_pool(name="keep", bufs=1))
         psum = ctx.enter_context(tc.psum_pool(name="psum", bufs=1))
 
-        offsets = keep.tile([P, (E * C) // 16], U16, name="offsets")
+        offsets = keep.tile([P, SLOTS // 16], U16, name="offsets")
         nc.sync.dma_start(offsets[:], offs)
 
         w_planes = keep.tile([P, E * PASSES, N], U8, name="w_planes", align_bytes=64)
@@ -35,7 +37,7 @@ def tile_routed_moe_kernel(tc, xT, w_words, w_scales, gate, offs, out):
 
         x_view = xT.rearrange("(g p t) n -> g p t n", p=P, t=PACK)
         raw = [keep.tile([P, PACK, T], F32, name="raw%d" % g) for g in range(PASSES)]
-        rounded = {g: keep.tile([P, PACK, T], BF16, name="rounded%d" % g) for g in (1, 3)}
+        rounded = {g: keep.tile([P, planes, T], BF16, name="rounded%d" % g) for g, planes in ((1, 4), (3, 2))}
 
         def load(g, t):
             nc.sync.dma_start(raw[g][:, t, :], x_view[g, :, t, :])
@@ -43,9 +45,12 @@ def tile_routed_moe_kernel(tc, xT, w_words, w_scales, gate, offs, out):
         for t in range(PACK):
             load(0, t)
             load(1, t)
-        for g in (3, 2):
-            for t in range(PACK):
-                load(g, t)
+        load(3, 2)
+        load(3, 3)
+        for t in range(PACK):
+            load(2, t)
+        load(3, 0)
+        load(3, 1)
         s_view = w_scales.rearrange("e a (q i) n -> i q (e a) n", i=4)
         for i in range(4):
             nc.sync.dma_start(w_planes[i:P:32, :, :].bitcast(I32), s_view[i].bitcast(I32))
@@ -54,49 +59,43 @@ def tile_routed_moe_kernel(tc, xT, w_words, w_scales, gate, offs, out):
             wq = keep.tile([P, E, N], U32, name="w_codes%d" % a, align_bytes=64)
             nc.sync.dma_start(wq[:].bitcast(I32), w_words[:, a].rearrange("e p n r -> p e (n r)").bitcast(I32))
             w_codes.append(wq)
-        gate_sb = keep.tile([P, E * C], F32, name="gate_sb")
+        gate_sb = keep.tile([P, SLOTS], F32, name="gate_sb")
         nc.sync.dma_start(gate_sb[:], gate)
 
         acc = [psum.tile([N, C], F32, name="acc%d" % e) for e in range(E)]
-        sums = [keep.tile([N, PIECE], F32, name="sums%d" % s) for s in range((E * C) // PIECE)]
+        sums = [keep.tile([N, PIECE], F32, name="sums%d" % s) for s in range(SLOTS // PIECE)]
         window = keep.tile([N, T], F32, name="window")
 
-        grouped = {}
+        first_pass = keep.tile([P, 2, HALF, PACK], BF16, name="first_pass", align_bytes=64)
+        middle = [keep.tile([P, 2, HALF, PACK], BF16, name="middle%d" % h, align_bytes=64) for h in range(2)]
+        last_pass = [keep.tile([P, HALF, PACK], BF16, name="last_pass%d" % h, align_bytes=64) for h in range(2)]
 
-        def target(g, first, width, t):
-            if (g, first) not in grouped:
-                grouped[(g, first)] = keep.tile([P, width, PACK], BF16, name="grouped%d_%d" % (g, first), align_bytes=64)
-            return grouped[(g, first)][:, :, t]
+        def half_of_list(h):
+            return offsets[:, h * (HALF // 16) : (h + 1) * (HALF // 16)]
 
-        def vector_gather(g, first, width, t):
-            nc.vector.tensor_copy(
-                target(g, first, width, t),
-                raw[g][:, t, :].indirect(offsets[:, first // 16 : (first + width) // 16]),
-            )
+        def vector_gather(dst, g, t, h):
+            nc.vector.tensor_copy(dst, raw[g][:, t, :].indirect(half_of_list(h)))
 
-        def scalar_gather(g, first, width, t):
-            nc.scalar.activation(
-                target(g, first, width, t),
-                rounded[g][:, t, :].indirect(offsets[:, first // 16 : (first + width) // 16]),
-                COPY,
-            )
+        def scalar_gather(dst, g, t, h):
+            nc.scalar.activation(dst, rounded[g][:, t, :].indirect(half_of_list(h)), COPY)
 
-        def quantise_and_multiply(g, first, width):
-            codes = keep.tile([P, width], U32, name="codes%d_%d" % (g, first), align_bytes=64)
-            scales = keep.tile([P, width], U8, name="scales%d_%d" % (g, first), align_bytes=64)
-            nc.vector.quantize_mx(
-                out=codes[:].bitcast(FP8X4),
-                scales=scales[:],
-                in_=grouped[(g, first)][:].rearrange("p c t -> p (c t)"),
-            )
-            for j in range(width // C):
-                e = first // C + j
+        def quantise(values, slots, label):
+            codes = keep.tile([P, slots], U32, name="codes_" + label, align_bytes=64)
+            scales = keep.tile([P, slots], U8, name="scales_" + label, align_bytes=64)
+            nc.vector.quantize_mx(out=codes[:].bitcast(FP8X4), scales=scales[:], in_=values)
+            return codes, scales
+
+        def multiply(g, h, quantised, column):
+            codes, scales = quantised
+            for j in range(HALF // C):
+                e = h * (HALF // C) + j
+                cols = slice(column + j * C, column + (j + 1) * C)
                 nc.tensor.matmul_mx(
                     out=acc[e][:],
                     lhsT=w_codes[g][:, e, :].bitcast(FP8X4),
                     lhsT_scale=w_planes[:, e * PASSES + g, :],
-                    rhs=codes[:, j * C : (j + 1) * C].bitcast(FP8X4),
-                    rhs_scale=scales[:, j * C : (j + 1) * C],
+                    rhs=codes[:, cols].bitcast(FP8X4),
+                    rhs_scale=scales[:, cols],
                     start=(g == 0),
                     stop=(g == PASSES - 1),
                 )
@@ -115,40 +114,34 @@ def tile_routed_moe_kernel(tc, xT, w_words, w_scales, gate, offs, out):
             )
 
         for t in range(PACK):
-            vector_gather(0, 0, 512, t)
-            vector_gather(0, 512, 512, t)
+            for h in range(2):
+                vector_gather(first_pass[:, h, :, t], 0, t, h)
             nc.scalar.copy(rounded[1][:, t, :], raw[1][:, t, :])
-            scalar_gather(1, 0, 512, t)
-            scalar_gather(1, 512, 512, t)
-        nc.vector.tensor_copy(rounded[3][:, 0, :], raw[3][:, 0, :])
-        quantise_and_multiply(0, 0, 512)
-        nc.vector.tensor_copy(rounded[3][:, 1, :], raw[3][:, 1, :])
-        quantise_and_multiply(0, 512, 512)
-        nc.vector.tensor_copy(rounded[3][:, 2, :], raw[3][:, 2, :])
-        nc.vector.tensor_copy(rounded[3][:, 3, :], raw[3][:, 3, :])
+            for h in range(2):
+                scalar_gather(middle[h][:, 1, :, t], 1, t, h)
+        q0 = quantise(first_pass[:].rearrange("p h c t -> p (h c t)"), 2 * HALF, "0")
+        for h in range(2):
+            multiply(0, h, q0, h * HALF)
+        for t in (2, 3):
+            for h in range(2):
+                vector_gather(last_pass[h][:, :, t], 3, t, h)
         for t in range(PACK):
-            vector_gather(2, 0, 512, t)
-            scalar_gather(3, 0, 512, t)
-        quantise_and_multiply(1, 0, 512)
-        quantise_and_multiply(1, 512, 512)
-        vector_gather(2, 512, 512, 0)
-        quantise_and_multiply(2, 0, 512)
-        for t in range(1, PACK):
-            vector_gather(2, 512, 512, t)
-        for t in range(PACK):
-            scalar_gather(3, 512, 256, t)
-        quantise_and_multiply(3, 0, 512)
-        way_back_copy(0)
-        way_back_copy(1)
-        quantise_and_multiply(2, 512, 512)
-        scatter(0)
-        for t in range(PACK):
-            scalar_gather(3, 768, 256, t)
-        scatter(1)
-        quantise_and_multiply(3, 512, 256)
-        way_back_copy(2)
-        quantise_and_multiply(3, 768, 256)
-        way_back_copy(3)
-        scatter(2)
-        scatter(3)
+            for h in range(2):
+                vector_gather(middle[h][:, 0, :, t], 2, t, h)
+        for t in range(2):
+            nc.scalar.copy(rounded[3][:, t, :], raw[3][:, t, :])
+        for h in range(2):
+            for t in range(2):
+                scalar_gather(last_pass[h][:, :, t], 3, t, h)
+        for h in range(2):
+            q21 = quantise(middle[h][:].rearrange("p a c t -> p (a c t)"), 2 * HALF, "21_%d" % h)
+            multiply(2, h, q21, 0)
+            multiply(1, h, q21, HALF)
+        for h in range(2):
+            q3 = quantise(last_pass[h][:].rearrange("p c t -> p (c t)"), HALF, "3_%d" % h)
+            multiply(3, h, q3, 0)
+            way_back_copy(2 * h)
+            way_back_copy(2 * h + 1)
+        for s in range(SLOTS // PIECE):
+            scatter(s)
         nc.sync.dma_start(out, window[:])

@@ -20,7 +20,6 @@ PACK = 4
 PASSES = K // (P * PACK)
 SLOTS = E * C
 HALF = 512
-PIECE = 256
 
 
 def tile_routed_moe_kernel(tc, xT, w_words, w_scales, gate, offs, out):
@@ -36,11 +35,15 @@ def tile_routed_moe_kernel(tc, xT, w_words, w_scales, gate, offs, out):
         nc.vector.memset(w_planes[:].rearrange("p g n -> p (g n)").bitcast(I32), 0)
 
         x_view = xT.rearrange("(g p t) n -> g p t n", p=P, t=PACK)
-        raw = [keep.tile([P, PACK, T], F32, name="raw%d" % g) for g in range(PASSES)]
+        plane = {(g, t): keep.tile([P, T], F32, name="plane%d_%d" % (g, t)) for g in (0, 2) for t in range(PACK)}
+        raw = {g: keep.tile([P, PACK, T], F32, name="raw%d" % g) for g in (1, 3)}
         rounded = {g: keep.tile([P, planes, T], BF16, name="rounded%d" % g) for g, planes in ((1, 4), (3, 2))}
 
         def load(g, t):
-            nc.sync.dma_start(raw[g][:, t, :], x_view[g, :, t, :])
+            if g in raw:
+                nc.sync.dma_start(raw[g][:, t, :], x_view[g, :, t, :])
+            else:
+                nc.sync.dma_start(plane[(g, t)][:], x_view[g, :, t, :])
 
         for t in range(PACK):
             load(0, t)
@@ -63,15 +66,18 @@ def tile_routed_moe_kernel(tc, xT, w_words, w_scales, gate, offs, out):
         nc.sync.dma_start(gate_sb[:], gate)
 
         acc = [psum.tile([N, C], F32, name="acc%d" % e) for e in range(E)]
-        sums = [keep.tile([N, PIECE], F32, name="sums%d" % s) for s in range(SLOTS // PIECE)]
+        sums = [keep.tile([N, HALF], F32, name="sums%d" % h) for h in range(2)]
         window = keep.tile([N, T], F32, name="window")
 
-        first_pass = keep.tile([P, 2, HALF, PACK], BF16, name="first_pass", align_bytes=64)
+        gathered = {(g, h): keep.tile([P, PACK, HALF], F32, name="gathered%d_%d" % (g, h)) for g in (0, 2) for h in range(2)}
         middle = [keep.tile([P, 2, HALF, PACK], BF16, name="middle%d" % h, align_bytes=64) for h in range(2)]
-        last_pass = [keep.tile([P, HALF, PACK], BF16, name="last_pass%d" % h, align_bytes=64) for h in range(2)]
+        outer = [keep.tile([P, 2, HALF, PACK], BF16, name="outer%d" % h, align_bytes=64) for h in range(2)]
 
         def half_of_list(h):
             return offsets[:, h * (HALF // 16) : (h + 1) * (HALF // 16)]
+
+        def gather_plane(g, t, h):
+            nc.vector.tensor_copy(gathered[(g, h)][:, t, :], plane[(g, t)][:].indirect(half_of_list(h)))
 
         def vector_gather(dst, g, t, h):
             nc.vector.tensor_copy(dst, raw[g][:, t, :].indirect(half_of_list(h)))
@@ -79,13 +85,15 @@ def tile_routed_moe_kernel(tc, xT, w_words, w_scales, gate, offs, out):
         def scalar_gather(dst, g, t, h):
             nc.scalar.activation(dst, rounded[g][:, t, :].indirect(half_of_list(h)), COPY)
 
-        def quantise(values, slots, label):
-            codes = keep.tile([P, slots], U32, name="codes_" + label, align_bytes=64)
-            scales = keep.tile([P, slots], U8, name="scales_" + label, align_bytes=64)
-            nc.vector.quantize_mx(out=codes[:].bitcast(FP8X4), scales=scales[:], in_=values)
+        def quantise(values, label):
+            codes = keep.tile([P, 2 * HALF], U32, name="codes_" + label, align_bytes=64)
+            scales = keep.tile([P, 2 * HALF], U8, name="scales_" + label, align_bytes=64)
+            nc.vector.quantize_mx(
+                out=codes[:].bitcast(FP8X4), scales=scales[:], in_=values[:].rearrange("p a c t -> p (a c t)")
+            )
             return codes, scales
 
-        def multiply(g, h, quantised, column):
+        def multiply(g, h, quantised, column, start, stop):
             codes, scales = quantised
             for j in range(HALF // C):
                 e = h * (HALF // C) + j
@@ -96,52 +104,43 @@ def tile_routed_moe_kernel(tc, xT, w_words, w_scales, gate, offs, out):
                     lhsT_scale=w_planes[:, e * PASSES + g, :],
                     rhs=codes[:, cols].bitcast(FP8X4),
                     rhs_scale=scales[:, cols],
-                    start=(g == 0),
-                    stop=(g == PASSES - 1),
+                    start=start,
+                    stop=stop,
                 )
-
-        def way_back_copy(s):
-            for j in range(PIECE // C):
-                nc.scalar.copy(sums[s][:, j * C : (j + 1) * C], acc[s * (PIECE // C) + j][:])
-
-        def scatter(s):
-            first = s * PIECE
-            nc.vector.tensor_tensor(
-                window[:].indirect(offsets[:, first // 16 : (first + PIECE) // 16]),
-                sums[s][:],
-                gate_sb[:, first : first + PIECE],
-                MULT,
-            )
 
         for t in range(PACK):
             for h in range(2):
-                vector_gather(first_pass[:, h, :, t], 0, t, h)
+                gather_plane(0, t, h)
             nc.scalar.copy(rounded[1][:, t, :], raw[1][:, t, :])
             for h in range(2):
                 scalar_gather(middle[h][:, 1, :, t], 1, t, h)
-        q0 = quantise(first_pass[:].rearrange("p h c t -> p (h c t)"), 2 * HALF, "0")
         for h in range(2):
-            multiply(0, h, q0, h * HALF)
+            nc.scalar.copy(outer[h][:, 0, :, :], gathered[(0, h)][:].rearrange("p t c -> p c t"))
         for t in (2, 3):
             for h in range(2):
-                vector_gather(last_pass[h][:, :, t], 3, t, h)
+                vector_gather(outer[h][:, 1, :, t], 3, t, h)
         for t in range(PACK):
             for h in range(2):
-                vector_gather(middle[h][:, 0, :, t], 2, t, h)
+                gather_plane(2, t, h)
+        for h in range(2):
+            nc.vector.tensor_copy(middle[h][:, 0, :, :], gathered[(2, h)][:].rearrange("p t c -> p c t"))
         for t in range(2):
             nc.scalar.copy(rounded[3][:, t, :], raw[3][:, t, :])
         for h in range(2):
             for t in range(2):
-                scalar_gather(last_pass[h][:, :, t], 3, t, h)
+                scalar_gather(outer[h][:, 1, :, t], 3, t, h)
         for h in range(2):
-            q21 = quantise(middle[h][:].rearrange("p a c t -> p (a c t)"), 2 * HALF, "21_%d" % h)
-            multiply(2, h, q21, 0)
-            multiply(1, h, q21, HALF)
+            q21 = quantise(middle[h], "21_%d" % h)
+            multiply(2, h, q21, 0, True, False)
+            multiply(1, h, q21, HALF, False, False)
         for h in range(2):
-            q3 = quantise(last_pass[h][:].rearrange("p c t -> p (c t)"), HALF, "3_%d" % h)
-            multiply(3, h, q3, 0)
-            way_back_copy(2 * h)
-            way_back_copy(2 * h + 1)
-        for s in range(SLOTS // PIECE):
-            scatter(s)
+            q03 = quantise(outer[h], "03_%d" % h)
+            multiply(0, h, q03, 0, False, False)
+            multiply(3, h, q03, HALF, False, True)
+            for j in range(HALF // C):
+                nc.scalar.copy(sums[h][:, j * C : (j + 1) * C], acc[h * (HALF // C) + j][:])
+        for h in range(2):
+            nc.vector.tensor_tensor(
+                window[:].indirect(half_of_list(h)), sums[h][:], gate_sb[:, h * HALF : (h + 1) * HALF], MULT
+            )
         nc.sync.dma_start(out, window[:])

@@ -35,15 +35,11 @@ def tile_routed_moe_kernel(tc, xT, w_words, w_scales, gate, offs, out):
         nc.vector.memset(w_planes[:].rearrange("p g n -> p (g n)").bitcast(I32), 0)
 
         x_view = xT.rearrange("(g p t) n -> g p t n", p=P, t=PACK)
-        plane = {(g, t): keep.tile([P, T], F32, name="plane%d_%d" % (g, t)) for g in (0, 2) for t in range(PACK)}
-        raw = {g: keep.tile([P, PACK, T], F32, name="raw%d" % g) for g in (1, 3)}
+        raw = [keep.tile([P, PACK, T], F32, name="raw%d" % g) for g in range(PASSES)]
         rounded = {g: keep.tile([P, planes, T], BF16, name="rounded%d" % g) for g, planes in ((1, 4), (3, 2))}
 
         def load(g, t):
-            if g in raw:
-                nc.sync.dma_start(raw[g][:, t, :], x_view[g, :, t, :])
-            else:
-                nc.sync.dma_start(plane[(g, t)][:], x_view[g, :, t, :])
+            nc.sync.dma_start(raw[g][:, t, :], x_view[g, :, t, :])
 
         for t in range(PACK):
             load(0, t)
@@ -69,7 +65,7 @@ def tile_routed_moe_kernel(tc, xT, w_words, w_scales, gate, offs, out):
         sums = [keep.tile([N, HALF], F32, name="sums%d" % h) for h in range(2)]
         window = keep.tile([N, T], F32, name="window")
 
-        gathered = {(g, h): keep.tile([P, PACK, HALF], F32, name="gathered%d_%d" % (g, h)) for g in (0, 2) for h in range(2)}
+        pairs = {(g, h): keep.tile([P, 2, HALF, 2], BF16, name="pairs%d_%d" % (g, h), align_bytes=64) for g in (0, 2) for h in range(2)}
         middle = [keep.tile([P, 2, HALF, PACK], BF16, name="middle%d" % h, align_bytes=64) for h in range(2)]
         outer = [keep.tile([P, 2, HALF, PACK], BF16, name="outer%d" % h, align_bytes=64) for h in range(2)]
 
@@ -77,7 +73,10 @@ def tile_routed_moe_kernel(tc, xT, w_words, w_scales, gate, offs, out):
             return offsets[:, h * (HALF // 16) : (h + 1) * (HALF // 16)]
 
         def gather_plane(g, t, h):
-            nc.vector.tensor_copy(gathered[(g, h)][:, t, :], plane[(g, t)][:].indirect(half_of_list(h)))
+            nc.vector.tensor_copy(pairs[(g, h)][:, t // 2, :, t % 2], raw[g][:, t, :].indirect(half_of_list(h)))
+
+        def merge(copy, dst, g, h):
+            copy(dst.bitcast(F32), pairs[(g, h)][:].bitcast(F32).rearrange("p u c o -> p c (u o)"))
 
         def vector_gather(dst, g, t, h):
             nc.vector.tensor_copy(dst, raw[g][:, t, :].indirect(half_of_list(h)))
@@ -93,20 +92,23 @@ def tile_routed_moe_kernel(tc, xT, w_words, w_scales, gate, offs, out):
             )
             return codes, scales
 
-        def multiply(g, h, quantised, column, start, stop):
+        def multiply(h, quantised, passes, opens, closes):
             codes, scales = quantised
             for j in range(HALF // C):
                 e = h * (HALF // C) + j
-                cols = slice(column + j * C, column + (j + 1) * C)
-                nc.tensor.matmul_mx(
-                    out=acc[e][:],
-                    lhsT=w_codes[g][:, e, :].bitcast(FP8X4),
-                    lhsT_scale=w_planes[:, e * PASSES + g, :],
-                    rhs=codes[:, cols].bitcast(FP8X4),
-                    rhs_scale=scales[:, cols],
-                    start=start,
-                    stop=stop,
-                )
+                for a, g in enumerate(passes):
+                    cols = slice(a * HALF + j * C, a * HALF + (j + 1) * C)
+                    nc.tensor.matmul_mx(
+                        out=acc[e][:],
+                        lhsT=w_codes[g][:, e, :].bitcast(FP8X4),
+                        lhsT_scale=w_planes[:, e * PASSES + g, :],
+                        rhs=codes[:, cols].bitcast(FP8X4),
+                        rhs_scale=scales[:, cols],
+                        start=(opens and a == 0),
+                        stop=(closes and a == 1),
+                    )
+                if closes:
+                    nc.scalar.copy(sums[h][:, j * C : (j + 1) * C], acc[e][:])
 
         for t in range(PACK):
             for h in range(2):
@@ -115,7 +117,7 @@ def tile_routed_moe_kernel(tc, xT, w_words, w_scales, gate, offs, out):
             for h in range(2):
                 scalar_gather(middle[h][:, 1, :, t], 1, t, h)
         for h in range(2):
-            nc.scalar.copy(outer[h][:, 0, :, :], gathered[(0, h)][:].rearrange("p t c -> p c t"))
+            merge(nc.scalar.copy, outer[h][:, 0, :, :], 0, h)
         for t in (2, 3):
             for h in range(2):
                 vector_gather(outer[h][:, 1, :, t], 3, t, h)
@@ -123,22 +125,16 @@ def tile_routed_moe_kernel(tc, xT, w_words, w_scales, gate, offs, out):
             for h in range(2):
                 gather_plane(2, t, h)
         for h in range(2):
-            nc.vector.tensor_copy(middle[h][:, 0, :, :], gathered[(2, h)][:].rearrange("p t c -> p c t"))
+            merge(nc.vector.tensor_copy, middle[h][:, 0, :, :], 2, h)
         for t in range(2):
             nc.scalar.copy(rounded[3][:, t, :], raw[3][:, t, :])
         for h in range(2):
             for t in range(2):
                 scalar_gather(outer[h][:, 1, :, t], 3, t, h)
         for h in range(2):
-            q21 = quantise(middle[h], "21_%d" % h)
-            multiply(2, h, q21, 0, True, False)
-            multiply(1, h, q21, HALF, False, False)
+            multiply(h, quantise(middle[h], "21_%d" % h), (2, 1), True, False)
         for h in range(2):
-            q03 = quantise(outer[h], "03_%d" % h)
-            multiply(0, h, q03, 0, False, False)
-            multiply(3, h, q03, HALF, False, True)
-            for j in range(HALF // C):
-                nc.scalar.copy(sums[h][:, j * C : (j + 1) * C], acc[h * (HALF // C) + j][:])
+            multiply(h, quantise(outer[h], "03_%d" % h), (0, 3), False, True)
         for h in range(2):
             nc.vector.tensor_tensor(
                 window[:].indirect(half_of_list(h)), sums[h][:], gate_sb[:, h * HALF : (h + 1) * HALF], MULT

@@ -113,7 +113,7 @@ def tile_routed_moe_kernel(tc, xT, w_words, w_scales, gate, offs, out):
         for t in range(PACK):
             for h in range(2):
                 gather_plane(0, t, h)
-            nc.scalar.copy(rounded[1][:, t, :], raw[1][:, t, :])
+            nc.gpsimd.tensor_copy(rounded[1][:, t, :], raw[1][:, t, :])
             for h in range(2):
                 scalar_gather(middle[h][:, 1, :, t], 1, t, h)
         for h in range(2):
@@ -127,7 +127,7 @@ def tile_routed_moe_kernel(tc, xT, w_words, w_scales, gate, offs, out):
         for h in range(2):
             merge(nc.vector.tensor_copy, middle[h][:, 0, :, :], 2, h)
         for t in range(2):
-            nc.scalar.copy(rounded[3][:, t, :], raw[3][:, t, :])
+            nc.gpsimd.tensor_copy(rounded[3][:, t, :], raw[3][:, t, :])
         for h in range(2):
             for t in range(2):
                 scalar_gather(outer[h][:, 1, :, t], 3, t, h)

@@ -35,21 +35,14 @@ def tile_routed_moe_kernel(tc, xT, w_words, w_scales, gate, offs, out):
         nc.vector.memset(w_planes[:].rearrange("p g n -> p (g n)").bitcast(I32), 0)
 
         x_view = xT.rearrange("(g p t) n -> g p t n", p=P, t=PACK)
-        raw = [keep.tile([P, PACK, T], F32, name="raw%d" % g) for g in range(PASSES)]
-        rounded = {g: keep.tile([P, planes, T], BF16, name="rounded%d" % g) for g, planes in ((1, 4), (3, 2))}
+        raw = [keep.tile([P, PACK, T], F32, name="raw%d" % g, tag="raw%d" % g, align_bytes=64) for g in range(PASSES)]
+        rounded = {g: keep.tile([P, PACK, T], BF16, name="rounded%d" % g) for g in (1, 3)}
 
-        def load(g, t):
+        for g, t in (
+            (1, 0), (0, 0), (1, 1), (0, 1), (0, 2), (1, 2), (0, 3), (1, 3),
+            (2, 0), (2, 1), (3, 0), (3, 1), (2, 2), (3, 2), (3, 3), (2, 3),
+        ):
             nc.sync.dma_start(raw[g][:, t, :], x_view[g, :, t, :])
-
-        for t in range(PACK):
-            load(0, t)
-            load(1, t)
-        load(3, 2)
-        load(3, 3)
-        for t in range(PACK):
-            load(2, t)
-        load(3, 0)
-        load(3, 1)
         s_view = w_scales.rearrange("e a (q i) n -> i q (e a) n", i=4)
         for i in range(4):
             nc.sync.dma_start(w_planes[i:P:32, :, :].bitcast(I32), s_view[i].bitcast(I32))
@@ -62,12 +55,13 @@ def tile_routed_moe_kernel(tc, xT, w_words, w_scales, gate, offs, out):
         nc.sync.dma_start(gate_sb[:], gate)
 
         acc = [psum.tile([N, C], F32, name="acc%d" % e) for e in range(E)]
-        sums = [keep.tile([N, HALF], F32, name="sums%d" % h) for h in range(2)]
+        sums = [keep.tile([N, HALF], F32, name="sums%d" % h, tag="sums%d" % h, align_bytes=64) for h in range(2)]
         window = keep.tile([N, T], F32, name="window")
 
-        pairs = {(g, h): keep.tile([P, 2, HALF, 2], BF16, name="pairs%d_%d" % (g, h), align_bytes=64) for g in (0, 2) for h in range(2)}
-        middle = [keep.tile([P, 2, HALF, PACK], BF16, name="middle%d" % h, align_bytes=64) for h in range(2)]
-        outer = [keep.tile([P, 2, HALF, PACK], BF16, name="outer%d" % h, align_bytes=64) for h in range(2)]
+        pairs = {(g, h): keep.tile([P, 2, HALF, 2], BF16, name="pairs%d_%d" % (g, h), tag="pairs%d_%d" % (g, h), align_bytes=64) for g in (0, 2) for h in range(2)}
+        first = keep.tile([P, 2, HALF, PACK], BF16, name="first", align_bytes=64)
+        middle = [keep.tile([P, 2, HALF, PACK], BF16, name="middle%d" % h, tag="middle%d" % h, align_bytes=64) for h in range(2)]
+        last = [keep.tile([P, HALF, PACK], BF16, name="last0", align_bytes=64)]
 
         def half_of_list(h):
             return offsets[:, h * (HALF // 16) : (h + 1) * (HALF // 16)]
@@ -75,67 +69,63 @@ def tile_routed_moe_kernel(tc, xT, w_words, w_scales, gate, offs, out):
         def gather_plane(g, t, h):
             nc.vector.tensor_copy(pairs[(g, h)][:, t // 2, :, t % 2], raw[g][:, t, :].indirect(half_of_list(h)))
 
-        def merge(copy, dst, g, h):
-            copy(dst.bitcast(F32), pairs[(g, h)][:].bitcast(F32).rearrange("p u c o -> p c (u o)"))
-
-        def vector_gather(dst, g, t, h):
-            nc.vector.tensor_copy(dst, raw[g][:, t, :].indirect(half_of_list(h)))
+        def merge(dst, g, h):
+            nc.gpsimd.tensor_copy(dst.bitcast(F32), pairs[(g, h)][:].bitcast(F32).rearrange("p u c o -> p c (u o)"))
 
         def scalar_gather(dst, g, t, h):
             nc.scalar.activation(dst, rounded[g][:, t, :].indirect(half_of_list(h)), COPY)
 
-        def quantise(values, label):
-            codes = keep.tile([P, 2 * HALF], U32, name="codes_" + label, align_bytes=64)
-            scales = keep.tile([P, 2 * HALF], U8, name="scales_" + label, align_bytes=64)
-            nc.vector.quantize_mx(
-                out=codes[:].bitcast(FP8X4), scales=scales[:], in_=values[:].rearrange("p a c t -> p (a c t)")
-            )
+        def quantise(values, slots, label, tag):
+            codes = keep.tile([P, slots], U32, name="codes_" + label, tag=tag, align_bytes=64)
+            scales = keep.tile([P, slots], U8, name="scales_" + label, align_bytes=64)
+            nc.vector.quantize_mx(out=codes[:].bitcast(FP8X4), scales=scales[:], in_=values)
             return codes, scales
 
-        def multiply(h, quantised, passes, opens, closes):
+        def multiply(experts, quantised, passes, opens, closes, empty):
             codes, scales = quantised
-            for j in range(HALF // C):
-                e = h * (HALF // C) + j
+            for j, e in enumerate(experts):
                 for a, g in enumerate(passes):
-                    cols = slice(a * HALF + j * C, a * HALF + (j + 1) * C)
+                    cols = slice((a * len(experts) + j) * C, (a * len(experts) + j + 1) * C)
                     nc.tensor.matmul_mx(
                         out=acc[e][:],
                         lhsT=w_codes[g][:, e, :].bitcast(FP8X4),
                         lhsT_scale=w_planes[:, e * PASSES + g, :],
                         rhs=codes[:, cols].bitcast(FP8X4),
                         rhs_scale=scales[:, cols],
-                        start=(opens and a == 0),
-                        stop=(closes and a == 1),
+                        start=opens,
+                        stop=closes,
                     )
                 if closes:
-                    nc.scalar.copy(sums[h][:, j * C : (j + 1) * C], acc[e][:])
+                    empty(sums[e // (HALF // C)][:, j * C : (j + 1) * C], acc[e][:])
+
+        def experts_of(h):
+            return list(range(h * (HALF // C), (h + 1) * (HALF // C)))
 
         for t in range(PACK):
-            for h in range(2):
-                gather_plane(0, t, h)
-            nc.gpsimd.tensor_copy(rounded[1][:, t, :], raw[1][:, t, :])
+            (nc.vector.tensor_copy if t == 0 else nc.gpsimd.tensor_copy)(rounded[1][:, t, :], raw[1][:, t, :])
             for h in range(2):
                 scalar_gather(middle[h][:, 1, :, t], 1, t, h)
-        for h in range(2):
-            merge(nc.scalar.copy, outer[h][:, 0, :, :], 0, h)
-        for t in (2, 3):
             for h in range(2):
-                vector_gather(outer[h][:, 1, :, t], 3, t, h)
+                gather_plane(0, t, h)
+        for h in range(2):
+            merge(first[:, h, :, :], 0, h)
+        for t in range(PACK):
+            nc.gpsimd.tensor_copy(rounded[3][:, t, :], raw[3][:, t, :])
+        for t in range(PACK):
+            scalar_gather(last[0][:, :, t], 3, t, 0)
         for t in range(PACK):
             for h in range(2):
                 gather_plane(2, t, h)
         for h in range(2):
-            merge(nc.vector.tensor_copy, middle[h][:, 0, :, :], 2, h)
-        for t in range(2):
-            nc.gpsimd.tensor_copy(rounded[3][:, t, :], raw[3][:, t, :])
+            merge(middle[h][:, 0, :, :], 2, h)
+        last.append(keep.tile([P, HALF, PACK], BF16, name="last1", tag="pairs2_0", align_bytes=64))
+        for t in range(PACK):
+            scalar_gather(last[1][:, :, t], 3, t, 1)
+        multiply(list(range(E)), quantise(first[:].rearrange("p h c t -> p (h c t)"), SLOTS, "0", "raw2"), (0,), True, False, None)
         for h in range(2):
-            for t in range(2):
-                scalar_gather(outer[h][:, 1, :, t], 3, t, h)
+            multiply(experts_of(h), quantise(middle[h][:].rearrange("p a c t -> p (a c t)"), 2 * HALF, "21_%d" % h, "codes_21_%d" % h), (2, 1), False, False, None)
         for h in range(2):
-            multiply(h, quantise(middle[h], "21_%d" % h), (2, 1), True, False)
-        for h in range(2):
-            multiply(h, quantise(outer[h], "03_%d" % h), (0, 3), False, True)
-        for h in range(2):
+            multiply(experts_of(h), quantise(last[h][:].rearrange("p c t -> p (c t)"), HALF, "3_%d" % h, ("middle1", "sums0")[h]), (3,), False, True, (nc.vector.tensor_copy, nc.scalar.copy)[h])
             nc.vector.tensor_tensor(
                 window[:].indirect(half_of_list(h)), sums[h][:], gate_sb[:, h * HALF : (h + 1) * HALF], MULT
             )

@@ -39,26 +39,30 @@ def tile_routed_moe_kernel(tc, xT, w_words, w_scales, gate, offs, out):
         rounded = {g: keep.tile([P, PACK, T], BF16, name="rounded%d" % g) for g in (1, 3)}
 
         for g, t in (
-            (1, 0), (0, 0), (1, 1), (0, 1), (0, 2), (1, 2), (0, 3), (1, 3),
-            (2, 0), (2, 1), (3, 0), (3, 1), (2, 2), (3, 2), (3, 3), (2, 3),
+            (0, 0), (1, 0), (0, 1), (1, 1), (0, 2), (1, 2), (0, 3), (1, 3),
+            (2, 0), (2, 1), (3, 0), (2, 2), (3, 1), (3, 2), (3, 3), (2, 3),
         ):
             nc.sync.dma_start(raw[g][:, t, :], x_view[g, :, t, :])
         s_view = w_scales.rearrange("e a (q i) n -> i q (e a) n", i=4)
         for i in range(4):
             nc.sync.dma_start(w_planes[i:P:32, :, :].bitcast(I32), s_view[i].bitcast(I32))
-        w_codes = []
-        for a in range(PASSES):
-            wq = keep.tile([P, E, N], U32, name="w_codes%d" % a, align_bytes=64)
-            nc.sync.dma_start(wq[:].bitcast(I32), w_words[:, a].rearrange("e p n r -> p e (n r)").bitcast(I32))
-            w_codes.append(wq)
+        w_codes = [keep.tile([P, E, N], U32, name="w_codes%d" % a, align_bytes=64) for a in range(PASSES)]
         gate_sb = keep.tile([P, SLOTS], F32, name="gate_sb")
-        nc.sync.dma_start(gate_sb[:], gate)
+        for h in range(2):
+            first_e = h * (HALF // C)
+            for a in (0, 2, 1, 3):
+                nc.sync.dma_start(
+                    w_codes[a][:, first_e : first_e + HALF // C, :].bitcast(I32),
+                    w_words[first_e : first_e + HALF // C, a].rearrange("e p n r -> p e (n r)").bitcast(I32),
+                )
+            if h == 0:
+                nc.sync.dma_start(gate_sb[:], gate)
 
         acc = [psum.tile([N, C], F32, name="acc%d" % e) for e in range(E)]
         sums = [keep.tile([N, HALF], F32, name="sums%d" % h, tag="sums%d" % h, align_bytes=64) for h in range(2)]
         window = keep.tile([N, T], F32, name="window")
 
-        pairs = {(g, h): keep.tile([P, 2, HALF, 2], BF16, name="pairs%d_%d" % (g, h), tag="pairs%d_%d" % (g, h), align_bytes=64) for g in (0, 2) for h in range(2)}
+        pairs = {g: keep.tile([P, 2, SLOTS, 2], BF16, name="pairs%d" % g, tag="pairs%d" % g, align_bytes=64) for g in (0, 2)}
         first = keep.tile([P, 2, HALF, PACK], BF16, name="first", align_bytes=64)
         middle = [keep.tile([P, 2, HALF, PACK], BF16, name="middle%d" % h, tag="middle%d" % h, align_bytes=64) for h in range(2)]
         last = [keep.tile([P, HALF, PACK], BF16, name="last0", align_bytes=64)]
@@ -66,11 +70,21 @@ def tile_routed_moe_kernel(tc, xT, w_words, w_scales, gate, offs, out):
         def half_of_list(h):
             return offsets[:, h * (HALF // 16) : (h + 1) * (HALF // 16)]
 
-        def gather_plane(g, t, h):
-            nc.vector.tensor_copy(pairs[(g, h)][:, t // 2, :, t % 2], raw[g][:, t, :].indirect(half_of_list(h)))
+        def gather_plane(g, t, whole):
+            if whole:
+                nc.vector.tensor_copy(
+                    pairs[g][:, t // 2, :, t % 2], raw[g][:, t : t + 2, :].rearrange("p a n -> p (a n)").indirect(offsets[:])
+                )
+            else:
+                for h in range(2):
+                    nc.vector.tensor_copy(
+                        pairs[g][:, t // 2, h * HALF : (h + 1) * HALF, t % 2], raw[g][:, t, :].indirect(half_of_list(h))
+                    )
 
         def merge(dst, g, h):
-            nc.gpsimd.tensor_copy(dst.bitcast(F32), pairs[(g, h)][:].bitcast(F32).rearrange("p u c o -> p c (u o)"))
+            nc.gpsimd.tensor_copy(
+                dst.bitcast(F32), pairs[g][:].bitcast(F32)[:, :, h * HALF : (h + 1) * HALF, :].rearrange("p u c o -> p c (u o)")
+            )
 
         def scalar_gather(dst, g, t, h):
             nc.scalar.activation(dst, rounded[g][:, t, :].indirect(half_of_list(h)), COPY)
@@ -102,11 +116,10 @@ def tile_routed_moe_kernel(tc, xT, w_words, w_scales, gate, offs, out):
             return list(range(h * (HALF // C), (h + 1) * (HALF // C)))
 
         for t in range(PACK):
-            (nc.vector.tensor_copy if t == 0 else nc.gpsimd.tensor_copy)(rounded[1][:, t, :], raw[1][:, t, :])
+            gather_plane(0, t, False)
+            nc.gpsimd.tensor_copy(rounded[1][:, t, :], raw[1][:, t, :])
             for h in range(2):
                 scalar_gather(middle[h][:, 1, :, t], 1, t, h)
-            for h in range(2):
-                gather_plane(0, t, h)
         for h in range(2):
             merge(first[:, h, :, :], 0, h)
         for t in range(PACK):
@@ -114,11 +127,10 @@ def tile_routed_moe_kernel(tc, xT, w_words, w_scales, gate, offs, out):
         for t in range(PACK):
             scalar_gather(last[0][:, :, t], 3, t, 0)
         for t in range(PACK):
-            for h in range(2):
-                gather_plane(2, t, h)
+            gather_plane(2, t, t < 2)
         for h in range(2):
             merge(middle[h][:, 0, :, :], 2, h)
-        last.append(keep.tile([P, HALF, PACK], BF16, name="last1", tag="pairs2_0", align_bytes=64))
+        last.append(keep.tile([P, HALF, PACK], BF16, name="last1", tag="raw3", align_bytes=64))
         for t in range(PACK):
             scalar_gather(last[1][:, :, t], 3, t, 1)
         multiply(list(range(E)), quantise(first[:].rearrange("p h c t -> p (h c t)"), SLOTS, "0", "raw2"), (0,), True, False, None)

@@ -59,16 +59,18 @@ def tile_routed_moe_kernel(tc, xT, w_words, w_scales, gate, offs, out):
                 nc.sync.dma_start(gate_sb[:], gate)
 
         acc = [psum.tile([N, C], F32, name="acc%d" % e) for e in range(E)]
-        sums = [keep.tile([N, HALF], F32, name="sums%d" % h, tag="sums%d" % h, align_bytes=64) for h in range(2)]
         window = keep.tile([N, T], F32, name="window")
 
-        pairs = {g: keep.tile([P, 2, SLOTS, 2], BF16, name="pairs%d" % g, tag="pairs%d" % g, align_bytes=64) for g in (0, 2)}
+        pairs = {g: keep.tile([P, 2, SLOTS, 2], BF16, name="pairs%d" % g, align_bytes=64) for g in (0, 1, 2)}
+        pairs3 = [keep.tile([P, 2, HALF, 2], BF16, name="pairs3_0", align_bytes=64)]
         first = keep.tile([P, 2, HALF, PACK], BF16, name="first", align_bytes=64)
-        middle = [keep.tile([P, 2, HALF, PACK], BF16, name="middle%d" % h, tag="middle%d" % h, align_bytes=64) for h in range(2)]
-        last = [keep.tile([P, HALF, PACK], BF16, name="last0", align_bytes=64)]
+        last = [keep.tile([P, HALF, PACK], BF16, name="last0", tag="last", align_bytes=64)]
 
         def half_of_list(h):
             return offsets[:, h * (HALF // 16) : (h + 1) * (HALF // 16)]
+
+        def half(tile4, h):
+            return tile4[:, :, h * HALF : (h + 1) * HALF, :]
 
         def gather_plane(g, t, whole):
             if whole:
@@ -77,17 +79,13 @@ def tile_routed_moe_kernel(tc, xT, w_words, w_scales, gate, offs, out):
                 )
             else:
                 for h in range(2):
-                    nc.vector.tensor_copy(
-                        pairs[g][:, t // 2, h * HALF : (h + 1) * HALF, t % 2], raw[g][:, t, :].indirect(half_of_list(h))
-                    )
+                    nc.vector.tensor_copy(half(pairs[g], h)[:, t // 2, :, t % 2], raw[g][:, t, :].indirect(half_of_list(h)))
 
-        def merge(dst, g, h):
-            nc.gpsimd.tensor_copy(
-                dst.bitcast(F32), pairs[g][:].bitcast(F32)[:, :, h * HALF : (h + 1) * HALF, :].rearrange("p u c o -> p c (u o)")
-            )
+        def merge(dst, src, copy):
+            copy(dst.bitcast(F32), src.bitcast(F32).rearrange("p u c o -> p c (u o)"))
 
-        def scalar_gather(dst, g, t, h):
-            nc.scalar.activation(dst, rounded[g][:, t, :].indirect(half_of_list(h)), COPY)
+        def scalar_gather(dst4, g, t, h):
+            nc.scalar.activation(dst4[:, t // 2, :, t % 2], rounded[g][:, t, :].indirect(half_of_list(h)), COPY)
 
         def quantise(values, slots, label, tag):
             codes = keep.tile([P, slots], U32, name="codes_" + label, tag=tag, align_bytes=64)
@@ -95,7 +93,7 @@ def tile_routed_moe_kernel(tc, xT, w_words, w_scales, gate, offs, out):
             nc.vector.quantize_mx(out=codes[:].bitcast(FP8X4), scales=scales[:], in_=values)
             return codes, scales
 
-        def multiply(experts, quantised, passes, opens, closes, empty):
+        def multiply(experts, quantised, passes, opens, closes):
             codes, scales = quantised
             for j, e in enumerate(experts):
                 for a, g in enumerate(passes):
@@ -110,7 +108,7 @@ def tile_routed_moe_kernel(tc, xT, w_words, w_scales, gate, offs, out):
                         stop=closes,
                     )
                 if closes:
-                    empty(sums[e // (HALF // C)][:, j * C : (j + 1) * C], acc[e][:])
+                    nc.scalar.copy(sums[e // (HALF // C)][:, j * C : (j + 1) * C], acc[e][:])
 
         def experts_of(h):
             return list(range(h * (HALF // C), (h + 1) * (HALF // C)))
@@ -119,25 +117,35 @@ def tile_routed_moe_kernel(tc, xT, w_words, w_scales, gate, offs, out):
             gather_plane(0, t, False)
             nc.gpsimd.tensor_copy(rounded[1][:, t, :], raw[1][:, t, :])
             for h in range(2):
-                scalar_gather(middle[h][:, 1, :, t], 1, t, h)
+                scalar_gather(half(pairs[1], h), 1, t, h)
         for h in range(2):
-            merge(first[:, h, :, :], 0, h)
+            merge(first[:, h, :, :], half(pairs[0], h), nc.gpsimd.tensor_copy)
         for t in range(PACK):
             nc.gpsimd.tensor_copy(rounded[3][:, t, :], raw[3][:, t, :])
         for t in range(PACK):
-            scalar_gather(last[0][:, :, t], 3, t, 0)
+            scalar_gather(pairs3[0][:], 3, t, 0)
         for t in range(PACK):
             gather_plane(2, t, t < 2)
-        for h in range(2):
-            merge(middle[h][:, 0, :, :], 2, h)
-        last.append(keep.tile([P, HALF, PACK], BF16, name="last1", tag="raw3", align_bytes=64))
+        late = keep.tile([P, 5, HALF, PACK], BF16, name="late", tag="raw3", align_bytes=64)
+        middle = [late[:, 2 * h : 2 * h + 2, :, :] for h in range(2)]
+        pairs3.append(late[:, 4, :, :].rearrange("p c t -> p (c t)").rearrange("p (u c e) -> p u c e", u=2, e=2))
+        for g in (1, 2):
+            for h in range(2):
+                merge(middle[h][:, 2 - g, :, :], half(pairs[g], h), nc.gpsimd.tensor_copy)
         for t in range(PACK):
-            scalar_gather(last[1][:, :, t], 3, t, 1)
-        multiply(list(range(E)), quantise(first[:].rearrange("p h c t -> p (h c t)"), SLOTS, "0", "raw2"), (0,), True, False, None)
+            scalar_gather(pairs3[1], 3, t, 1)
+        merge(last[0][:], pairs3[0], nc.gpsimd.tensor_copy)
+        multiply(list(range(E)), quantise(first[:].rearrange("p h c t -> p (h c t)"), SLOTS, "0", "raw2"), (0,), True, False)
         for h in range(2):
-            multiply(experts_of(h), quantise(middle[h][:].rearrange("p a c t -> p (a c t)"), 2 * HALF, "21_%d" % h, "codes_21_%d" % h), (2, 1), False, False, None)
+            multiply(experts_of(h), quantise(middle[h].rearrange("p a c t -> p (a c t)"), 2 * HALF, "21_%d" % h, "codes_21_%d" % h), (2, 1), False, False)
+        quantised3 = [quantise(last[0][:].rearrange("p c t -> p (c t)"), HALF, "3_0", "codes_3_0")]
+        last.append(keep.tile([P, HALF, PACK], BF16, name="last1", tag="last", align_bytes=64))
+        merge(last[1][:], pairs3[1], nc.vector.tensor_copy)
+        quantised3.append(quantise(last[1][:].rearrange("p c t -> p (c t)"), HALF, "3_1", "codes_3_1"))
+        sums = [keep.tile([N, HALF], F32, name="sums%d" % h, tag=("raw3", "sums1")[h], align_bytes=64) for h in range(2)]
         for h in range(2):
-            multiply(experts_of(h), quantise(last[h][:].rearrange("p c t -> p (c t)"), HALF, "3_%d" % h, ("middle1", "sums0")[h]), (3,), False, True, (nc.vector.tensor_copy, nc.scalar.copy)[h])
+            multiply(experts_of(h), quantised3[h], (3,), False, True)
+        for h in range(2):
             nc.vector.tensor_tensor(
                 window[:].indirect(half_of_list(h)), sums[h][:], gate_sb[:, h * HALF : (h + 1) * HALF], MULT
             )

@@ -35,14 +35,19 @@ def tile_routed_moe_kernel(tc, xT, w_words, w_scales, gate, offs, out):
         nc.vector.memset(w_planes[:].rearrange("p g n -> p (g n)").bitcast(I32), 0)
 
         x_view = xT.rearrange("(g p t) n -> g p t n", p=P, t=PACK)
-        raw = [keep.tile([P, PACK, T], F32, name="raw%d" % g, tag="raw%d" % g, align_bytes=64) for g in range(PASSES)]
+        raw = [keep.tile([P, PACK, T], F32, name="raw%d" % g, tag="raw%d" % g, align_bytes=64) for g in range(3)]
+        raw3 = [keep.tile([P, 2, T], F32, name="raw3_%d" % i, tag="raw3_%d" % i, align_bytes=64) for i in range(2)]
+
+        def plane(g, t):
+            return raw[g][:, t, :] if g < 3 else raw3[(0, 1, 1, 0)[t]][:, (0, 0, 1, 1)[t], :]
+
         rounded = {g: keep.tile([P, PACK, T], BF16, name="rounded%d" % g) for g in (1, 3)}
 
         for g, t in (
-            (0, 0), (1, 0), (0, 1), (1, 1), (0, 2), (1, 2), (0, 3), (1, 3),
+            (0, 0), (1, 0), (0, 1), (1, 1), (0, 2), (1, 2), (1, 3), (0, 3),
             (2, 0), (2, 1), (3, 0), (2, 2), (3, 1), (3, 2), (3, 3), (2, 3),
         ):
-            nc.sync.dma_start(raw[g][:, t, :], x_view[g, :, t, :])
+            nc.sync.dma_start(plane(g, t), x_view[g, :, t, :])
         s_view = w_scales.rearrange("e a (q i) n -> i q (e a) n", i=4)
         for i in range(4):
             nc.sync.dma_start(w_planes[i:P:32, :, :].bitcast(I32), s_view[i].bitcast(I32))
@@ -61,10 +66,9 @@ def tile_routed_moe_kernel(tc, xT, w_words, w_scales, gate, offs, out):
         acc = [psum.tile([N, C], F32, name="acc%d" % e) for e in range(E)]
         window = keep.tile([N, T], F32, name="window")
 
-        pairs = {g: keep.tile([P, 2, SLOTS, 2], BF16, name="pairs%d" % g, align_bytes=64) for g in (0, 1, 2)}
-        pairs3 = [keep.tile([P, 2, HALF, 2], BF16, name="pairs3_0", align_bytes=64)]
+        pairs = {g: keep.tile([P, 2, SLOTS, 2], BF16, name="pairs%d" % g, tag="pairs%d" % g, align_bytes=64) for g in (0, 1, 2)}
         first = keep.tile([P, 2, HALF, PACK], BF16, name="first", align_bytes=64)
-        last = [keep.tile([P, HALF, PACK], BF16, name="last0", tag="last", align_bytes=64)]
+        last = [keep.tile([P, HALF, PACK], BF16, name="last0", align_bytes=64)]
 
         def half_of_list(h):
             return offsets[:, h * (HALF // 16) : (h + 1) * (HALF // 16)]
@@ -84,8 +88,8 @@ def tile_routed_moe_kernel(tc, xT, w_words, w_scales, gate, offs, out):
         def merge(dst, src, copy):
             copy(dst.bitcast(F32), src.bitcast(F32).rearrange("p u c o -> p c (u o)"))
 
-        def scalar_gather(dst4, g, t, h):
-            nc.scalar.activation(dst4[:, t // 2, :, t % 2], rounded[g][:, t, :].indirect(half_of_list(h)), COPY)
+        def scalar_gather(dst, g, t, h):
+            nc.scalar.activation(dst, rounded[g][:, t, :].indirect(half_of_list(h)), COPY)
 
         def quantise(values, slots, label, tag):
             codes = keep.tile([P, slots], U32, name="codes_" + label, tag=tag, align_bytes=64)
@@ -117,32 +121,28 @@ def tile_routed_moe_kernel(tc, xT, w_words, w_scales, gate, offs, out):
             gather_plane(0, t, False)
             nc.gpsimd.tensor_copy(rounded[1][:, t, :], raw[1][:, t, :])
             for h in range(2):
-                scalar_gather(half(pairs[1], h), 1, t, h)
+                scalar_gather(half(pairs[1], h)[:, t // 2, :, t % 2], 1, t, h)
         for h in range(2):
             merge(first[:, h, :, :], half(pairs[0], h), nc.gpsimd.tensor_copy)
         for t in range(PACK):
-            nc.gpsimd.tensor_copy(rounded[3][:, t, :], raw[3][:, t, :])
+            nc.gpsimd.tensor_copy(rounded[3][:, t, :], plane(3, t))
         for t in range(PACK):
-            scalar_gather(pairs3[0][:], 3, t, 0)
+            scalar_gather(last[0][:, :, t], 3, t, 0)
         for t in range(PACK):
             gather_plane(2, t, t < 2)
-        late = keep.tile([P, 5, HALF, PACK], BF16, name="late", tag="raw3", align_bytes=64)
-        middle = [late[:, 2 * h : 2 * h + 2, :, :] for h in range(2)]
-        pairs3.append(late[:, 4, :, :].rearrange("p c t -> p (c t)").rearrange("p (u c e) -> p u c e", u=2, e=2))
-        for g in (1, 2):
-            for h in range(2):
-                merge(middle[h][:, 2 - g, :, :], half(pairs[g], h), nc.gpsimd.tensor_copy)
+        middle = keep.tile([P, 2, 2, HALF, PACK], BF16, name="middle", tag="raw3_1", align_bytes=64)
+        for h in range(2):
+            merge(middle[:, h, 1, :, :], half(pairs[1], h), nc.gpsimd.tensor_copy)
+        for h in range(2):
+            merge(middle[:, h, 0, :, :], half(pairs[2], h), nc.vector.tensor_copy)
+        last.append(keep.tile([P, HALF, PACK], BF16, name="last1", tag="raw3_0", align_bytes=64))
         for t in range(PACK):
-            scalar_gather(pairs3[1], 3, t, 1)
-        merge(last[0][:], pairs3[0], nc.gpsimd.tensor_copy)
+            scalar_gather(last[1][:, :, t], 3, t, 1)
         multiply(list(range(E)), quantise(first[:].rearrange("p h c t -> p (h c t)"), SLOTS, "0", "raw2"), (0,), True, False)
         for h in range(2):
-            multiply(experts_of(h), quantise(middle[h].rearrange("p a c t -> p (a c t)"), 2 * HALF, "21_%d" % h, "codes_21_%d" % h), (2, 1), False, False)
-        quantised3 = [quantise(last[0][:].rearrange("p c t -> p (c t)"), HALF, "3_0", "codes_3_0")]
-        last.append(keep.tile([P, HALF, PACK], BF16, name="last1", tag="last", align_bytes=64))
-        merge(last[1][:], pairs3[1], nc.vector.tensor_copy)
-        quantised3.append(quantise(last[1][:].rearrange("p c t -> p (c t)"), HALF, "3_1", "codes_3_1"))
-        sums = [keep.tile([N, HALF], F32, name="sums%d" % h, tag=("raw3", "sums1")[h], align_bytes=64) for h in range(2)]
+            multiply(experts_of(h), quantise(middle[:, h, :, :, :].rearrange("p a c t -> p (a c t)"), 2 * HALF, "21_%d" % h, "codes_21_%d" % h), (2, 1), False, False)
+        quantised3 = [quantise(last[h][:].rearrange("p c t -> p (c t)"), HALF, "3_%d" % h, ("codes_3_0", "raw3_1")[h]) for h in range(2)]
+        sums = [keep.tile([N, HALF], F32, name="sums%d" % h) for h in range(2)]
         for h in range(2):
             multiply(experts_of(h), quantised3[h], (3,), False, True)
         for h in range(2):

@@ -43,10 +43,10 @@ def tile_routed_moe_kernel(tc, xT, w_words, w_scales, gate, offs, out):
 
         rounded = {g: keep.tile([P, PACK, T], BF16, name="rounded%d" % g) for g in (1, 3)}
 
-        for g, t in (
-            (0, 0), (1, 0), (0, 1), (1, 1), (0, 2), (1, 2), (1, 3), (0, 3),
-            (2, 0), (2, 1), (3, 0), (2, 2), (3, 1), (3, 2), (3, 3), (2, 3),
-        ):
+        for g, t in ((0, 0), (1, 0), (0, 1), (1, 1), (0, 2), (1, 2), (1, 3), (0, 3)):
+            nc.sync.dma_start(plane(g, t), x_view[g, :, t, :])
+        nc.sync.dma_start(raw[2][:, 0:2, :], x_view[2, :, 0:2, :])
+        for g, t in ((3, 0), (2, 2), (3, 1), (3, 2), (3, 3), (2, 3)):
             nc.sync.dma_start(plane(g, t), x_view[g, :, t, :])
         s_view = w_scales.rearrange("e a (q i) n -> i q (e a) n", i=4)
         for i in range(4):
@@ -68,7 +68,7 @@ def tile_routed_moe_kernel(tc, xT, w_words, w_scales, gate, offs, out):
 
         pairs = {g: keep.tile([P, 2, SLOTS, 2], BF16, name="pairs%d" % g, tag="pairs%d" % g, align_bytes=64) for g in (0, 1, 2)}
         first = keep.tile([P, 2, HALF, PACK], BF16, name="first", align_bytes=64)
-        last = [keep.tile([P, HALF, PACK], BF16, name="last0", align_bytes=64)]
+        last = [keep.tile([P, HALF, PACK], BF16, name="last0", tag="last0", align_bytes=64)]
 
         def half_of_list(h):
             return offsets[:, h * (HALF // 16) : (h + 1) * (HALF // 16)]
@@ -135,13 +135,23 @@ def tile_routed_moe_kernel(tc, xT, w_words, w_scales, gate, offs, out):
             merge(middle[:, h, 1, :, :], half(pairs[1], h), nc.gpsimd.tensor_copy)
         for h in range(2):
             merge(middle[:, h, 0, :, :], half(pairs[2], h), nc.vector.tensor_copy)
-        last.append(keep.tile([P, HALF, PACK], BF16, name="last1", tag="raw3_0", align_bytes=64))
+        pairs3 = keep.tile([P, 2, HALF, 2], BF16, name="pairs3", tag="raw3_0", align_bytes=64)
         for t in range(PACK):
-            scalar_gather(last[1][:, :, t], 3, t, 1)
+            scalar_gather(pairs3[:, t // 2, :, t % 2], 3, t, 1)
+
+        def two_and_one(h, tag):
+            multiply(experts_of(h), quantise(middle[:, h, :, :, :].rearrange("p a c t -> p (a c t)"), 2 * HALF, "21_%d" % h, tag), (2, 1), False, False)
+
+        def three(h):
+            return quantise(last[h][:].rearrange("p c t -> p (c t)"), HALF, "3_%d" % h, "codes_3_%d" % h)
+
         multiply(list(range(E)), quantise(first[:].rearrange("p h c t -> p (h c t)"), SLOTS, "0", "raw2"), (0,), True, False)
-        for h in range(2):
-            multiply(experts_of(h), quantise(middle[:, h, :, :, :].rearrange("p a c t -> p (a c t)"), 2 * HALF, "21_%d" % h, "codes_21_%d" % h), (2, 1), False, False)
-        quantised3 = [quantise(last[h][:].rearrange("p c t -> p (c t)"), HALF, "3_%d" % h, ("codes_3_0", "raw3_1")[h]) for h in range(2)]
+        two_and_one(0, "codes_21_0")
+        quantised3 = [three(0)]
+        two_and_one(1, "last0")
+        last.append(keep.tile([P, HALF, PACK], BF16, name="last1", tag="raw3_1", align_bytes=64))
+        merge(last[1][:], pairs3[:], nc.vector.tensor_copy)
+        quantised3.append(three(1))
         sums = [keep.tile([N, HALF], F32, name="sums%d" % h) for h in range(2)]
         for h in range(2):
             multiply(experts_of(h), quantised3[h], (3,), False, True)

@@ -35,17 +35,23 @@ def tile_routed_moe_kernel(tc, xT, w_words, w_scales, gate, offs, out):
         nc.vector.memset(w_planes[:].rearrange("p g n -> p (g n)").bitcast(I32), 0)
 
         x_view = xT.rearrange("(g p t) n -> g p t n", p=P, t=PACK)
-        raw = [keep.tile([P, PACK, T], F32, name="raw%d" % g, tag="raw%d" % g, align_bytes=64) for g in range(3)]
+        place = {(2, 3): 0, (2, 2): 1, (2, 0): 2, (2, 1): 3, (0, 3): 4, (0, 2): 5, (0, 1): 6, (0, 0): 7}
+        raw02 = keep.tile([P, 2 * PACK, T], F32, name="raw02", tag="raw02", align_bytes=64)
+        raw1 = keep.tile([P, PACK, T], F32, name="raw1", tag="raw1", align_bytes=64)
         raw3 = [keep.tile([P, 2, T], F32, name="raw3_%d" % i, tag="raw3_%d" % i, align_bytes=64) for i in range(2)]
 
         def plane(g, t):
-            return raw[g][:, t, :] if g < 3 else raw3[(0, 1, 1, 0)[t]][:, (0, 0, 1, 1)[t], :]
+            if g == 1:
+                return raw1[:, t, :]
+            if g == 3:
+                return raw3[(0, 1, 1, 0)[t]][:, (0, 0, 1, 1)[t], :]
+            return raw02[:, place[(g, t)], :]
 
         rounded = {g: keep.tile([P, PACK, T], BF16, name="rounded%d" % g) for g in (1, 3)}
 
-        for g, t in ((0, 0), (1, 0), (0, 1), (1, 1), (0, 2), (1, 2), (1, 3), (0, 3)):
+        for g, t in ((0, 0), (1, 0), (0, 1), (1, 1), (0, 2), (1, 2), (0, 3), (1, 3)):
             nc.sync.dma_start(plane(g, t), x_view[g, :, t, :])
-        nc.sync.dma_start(raw[2][:, 0:2, :], x_view[2, :, 0:2, :])
+        nc.sync.dma_start(raw02[:, place[(2, 0)] : place[(2, 0)] + 2, :], x_view[2, :, 0:2, :])
         for g, t in ((3, 0), (2, 2), (3, 1), (3, 2), (3, 3), (2, 3)):
             nc.sync.dma_start(plane(g, t), x_view[g, :, t, :])
         s_view = w_scales.rearrange("e a (q i) n -> i q (e a) n", i=4)
@@ -67,7 +73,6 @@ def tile_routed_moe_kernel(tc, xT, w_words, w_scales, gate, offs, out):
         window = keep.tile([N, T], F32, name="window")
 
         pairs = {g: keep.tile([P, 2, SLOTS, 2], BF16, name="pairs%d" % g, tag="pairs%d" % g, align_bytes=64) for g in (0, 1, 2)}
-        first = keep.tile([P, 2, HALF, PACK], BF16, name="first", align_bytes=64)
         last = [keep.tile([P, HALF, PACK], BF16, name="last0", tag="last0", align_bytes=64)]
 
         def half_of_list(h):
@@ -78,12 +83,11 @@ def tile_routed_moe_kernel(tc, xT, w_words, w_scales, gate, offs, out):
 
         def gather_plane(g, t, whole):
             if whole:
-                nc.vector.tensor_copy(
-                    pairs[g][:, t // 2, :, t % 2], raw[g][:, t : t + 2, :].rearrange("p a n -> p (a n)").indirect(offsets[:])
-                )
+                two = raw02[:, place[(g, t)] : place[(g, t)] + 2, :].rearrange("p a n -> p (a n)")
+                nc.vector.tensor_copy(pairs[g][:, t // 2, :, t % 2], two.indirect(offsets[:]))
             else:
                 for h in range(2):
-                    nc.vector.tensor_copy(half(pairs[g], h)[:, t // 2, :, t % 2], raw[g][:, t, :].indirect(half_of_list(h)))
+                    nc.vector.tensor_copy(half(pairs[g], h)[:, t // 2, :, t % 2], plane(g, t).indirect(half_of_list(h)))
 
         def merge(dst, src, copy):
             copy(dst.bitcast(F32), src.bitcast(F32).rearrange("p u c o -> p c (u o)"))
@@ -118,10 +122,11 @@ def tile_routed_moe_kernel(tc, xT, w_words, w_scales, gate, offs, out):
             return list(range(h * (HALF // C), (h + 1) * (HALF // C)))
 
         for t in range(PACK):
-            gather_plane(0, t, False)
-            nc.gpsimd.tensor_copy(rounded[1][:, t, :], raw[1][:, t, :])
+            gather_plane(0, t, t in (1, 2))
+            nc.gpsimd.tensor_copy(rounded[1][:, t, :], plane(1, t))
             for h in range(2):
                 scalar_gather(half(pairs[1], h)[:, t // 2, :, t % 2], 1, t, h)
+        first = keep.tile([P, 2, HALF, PACK], BF16, name="first", tag="raw1", align_bytes=64)
         for h in range(2):
             merge(first[:, h, :, :], half(pairs[0], h), nc.gpsimd.tensor_copy)
         for t in range(PACK):
@@ -129,29 +134,30 @@ def tile_routed_moe_kernel(tc, xT, w_words, w_scales, gate, offs, out):
         for t in range(PACK):
             scalar_gather(last[0][:, :, t], 3, t, 0)
         for t in range(PACK):
-            gather_plane(2, t, t < 2)
+            gather_plane(2, t, True)
         middle = keep.tile([P, 2, 2, HALF, PACK], BF16, name="middle", tag="raw3_1", align_bytes=64)
         for h in range(2):
             merge(middle[:, h, 1, :, :], half(pairs[1], h), nc.gpsimd.tensor_copy)
-        for h in range(2):
-            merge(middle[:, h, 0, :, :], half(pairs[2], h), nc.vector.tensor_copy)
+        nc.vector.tensor_copy(
+            middle[:, :, 0, :, :].bitcast(F32), pairs[2][:].bitcast(F32).rearrange("p u (h c) o -> p h c (u o)", h=2)
+        )
         pairs3 = keep.tile([P, 2, HALF, 2], BF16, name="pairs3", tag="raw3_0", align_bytes=64)
         for t in range(PACK):
             scalar_gather(pairs3[:, t // 2, :, t % 2], 3, t, 1)
+        last.append(keep.tile([P, HALF, PACK], BF16, name="last1", align_bytes=64))
+        merge(last[1][:], pairs3[:], nc.scalar.copy)
 
         def two_and_one(h, tag):
             multiply(experts_of(h), quantise(middle[:, h, :, :, :].rearrange("p a c t -> p (a c t)"), 2 * HALF, "21_%d" % h, tag), (2, 1), False, False)
 
-        def three(h):
-            return quantise(last[h][:].rearrange("p c t -> p (c t)"), HALF, "3_%d" % h, "codes_3_%d" % h)
+        def three(h, tag):
+            return quantise(last[h][:].rearrange("p c t -> p (c t)"), HALF, "3_%d" % h, tag)
 
-        multiply(list(range(E)), quantise(first[:].rearrange("p h c t -> p (h c t)"), SLOTS, "0", "raw2"), (0,), True, False)
+        multiply(list(range(E)), quantise(first[:].rearrange("p h c t -> p (h c t)"), SLOTS, "0", "raw02"), (0,), True, False)
         two_and_one(0, "codes_21_0")
-        quantised3 = [three(0)]
+        quantised3 = [three(0, "codes_3_0")]
         two_and_one(1, "last0")
-        last.append(keep.tile([P, HALF, PACK], BF16, name="last1", tag="raw3_1", align_bytes=64))
-        merge(last[1][:], pairs3[:], nc.vector.tensor_copy)
-        quantised3.append(three(1))
+        quantised3.append(three(1, "raw3_1"))
         sums = [keep.tile([N, HALF], F32, name="sums%d" % h) for h in range(2)]
         for h in range(2):
             multiply(experts_of(h), quantised3[h], (3,), False, True)

@@ -101,7 +101,7 @@ def tile_routed_moe_kernel(tc, xT, w_words, w_scales, gate, offs, out):
             nc.vector.quantize_mx(out=codes[:].bitcast(FP8X4), scales=scales[:], in_=values)
             return codes, scales
 
-        def multiply(experts, quantised, passes, opens, closes):
+        def multiply(experts, quantised, passes, opens, sums=None):
             codes, scales = quantised
             for j, e in enumerate(experts):
                 for a, g in enumerate(passes):
@@ -113,10 +113,10 @@ def tile_routed_moe_kernel(tc, xT, w_words, w_scales, gate, offs, out):
                         rhs=codes[:, cols].bitcast(FP8X4),
                         rhs_scale=scales[:, cols],
                         start=opens,
-                        stop=closes,
+                        stop=sums is not None,
                     )
-                if closes:
-                    nc.scalar.copy(sums[e // (HALF // C)][:, j * C : (j + 1) * C], acc[e][:])
+                if sums is not None:
+                    nc.scalar.copy(sums[:, j * C : (j + 1) * C], acc[e][:])
 
         def experts_of(h):
             return list(range(h * (HALF // C), (h + 1) * (HALF // C)))
@@ -141,28 +141,43 @@ def tile_routed_moe_kernel(tc, xT, w_words, w_scales, gate, offs, out):
         nc.vector.tensor_copy(
             middle[:, :, 0, :, :].bitcast(F32), pairs[2][:].bitcast(F32).rearrange("p u (h c) o -> p h c (u o)", h=2)
         )
-        pairs3 = keep.tile([P, 2, HALF, 2], BF16, name="pairs3", tag="raw3_0", align_bytes=64)
-        for t in range(PACK):
-            scalar_gather(pairs3[:, t // 2, :, t % 2], 3, t, 1)
-        last.append(keep.tile([P, HALF, PACK], BF16, name="last1", align_bytes=64))
-        merge(last[1][:], pairs3[:], nc.scalar.copy)
+        QUARTER = HALF // 2
+
+        def quarter_of_list(q):
+            return offsets[:, (HALF + q * QUARTER) // 16 : (HALF + (q + 1) * QUARTER) // 16]
+
+        def late_quarter(q, tag):
+            pairs3 = keep.tile([P, 2, QUARTER, 2], BF16, name="pairs3_%d" % q, tag=tag, align_bytes=64)
+            for t in range(PACK):
+                nc.scalar.activation(pairs3[:, t // 2, :, t % 2], rounded[3][:, t, :].indirect(quarter_of_list(q)), COPY)
+            values = keep.tile([P, QUARTER, PACK], BF16, name="late%d" % q, align_bytes=64)
+            merge(values[:], pairs3[:], nc.scalar.copy)
+            return values
 
         def two_and_one(h, tag):
-            multiply(experts_of(h), quantise(middle[:, h, :, :, :].rearrange("p a c t -> p (a c t)"), 2 * HALF, "21_%d" % h, tag), (2, 1), False, False)
+            multiply(experts_of(h), quantise(middle[:, h, :, :, :].rearrange("p a c t -> p (a c t)"), 2 * HALF, "21_%d" % h, tag), (2, 1), False)
 
-        def three(h, tag):
-            return quantise(last[h][:].rearrange("p c t -> p (c t)"), HALF, "3_%d" % h, tag)
-
-        multiply(list(range(E)), quantise(first[:].rearrange("p h c t -> p (h c t)"), SLOTS, "0", "raw02"), (0,), True, False)
+        late = [late_quarter(0, "raw3_0")]
+        multiply(list(range(E)), quantise(first[:].rearrange("p h c t -> p (h c t)"), SLOTS, "0", "raw02"), (0,), True)
         two_and_one(0, "codes_21_0")
-        quantised3 = [three(0, "codes_3_0")]
+        quantised_a = quantise(last[0][:].rearrange("p c t -> p (c t)"), HALF, "3_a", "codes_3_a")
         two_and_one(1, "last0")
-        quantised3.append(three(1, "raw3_1"))
-        sums = [keep.tile([N, HALF], F32, name="sums%d" % h) for h in range(2)]
-        for h in range(2):
-            multiply(experts_of(h), quantised3[h], (3,), False, True)
-        for h in range(2):
+        quantised_b = quantise(late[0][:].rearrange("p c t -> p (c t)"), QUARTER, "3_b", "raw3_1")
+        sums_a = keep.tile([N, HALF], F32, name="sums_a", tag="sums_a", align_bytes=64)
+        multiply([0, 1, 2, 3], quantised_a, (3,), False, sums_a)
+        late.append(late_quarter(1, "codes_3_a"))
+        sums_b = keep.tile([N, QUARTER], F32, name="sums_b")
+        multiply([4, 5], quantised_b, (3,), False, sums_b)
+
+        def scatter(values, first_slot, slots):
             nc.vector.tensor_tensor(
-                window[:].indirect(half_of_list(h)), sums[h][:], gate_sb[:, h * HALF : (h + 1) * HALF], MULT
+                window[:].indirect(offsets[:, first_slot // 16 : (first_slot + slots) // 16]), values[:], gate_sb[:, first_slot : first_slot + slots], MULT
             )
+
+        scatter(sums_a, 0, HALF)
+        quantised_c = quantise(late[1][:].rearrange("p c t -> p (c t)"), QUARTER, "3_c", "sums_a")
+        sums_c = keep.tile([N, QUARTER], F32, name="sums_c")
+        multiply([6, 7], quantised_c, (3,), False, sums_c)
+        scatter(sums_b, HALF, QUARTER)
+        scatter(sums_c, HALF + QUARTER, QUARTER)
         nc.sync.dma_start(out, window[:])

@@ -161,8 +161,8 @@ def tile_routed_moe_kernel(tc, xT, w_words, w_scales, gate, offs, out):
         multiply(list(range(E)), quantise(first[:].rearrange("p h c t -> p (h c t)"), SLOTS, "0", "raw02"), (0,), True)
         two_and_one(0, "codes_21_0")
         quantised_a = quantise(last[0][:].rearrange("p c t -> p (c t)"), HALF, "3_a", "codes_3_a")
-        two_and_one(1, "last0")
-        quantised_b = quantise(late[0][:].rearrange("p c t -> p (c t)"), QUARTER, "3_b", "raw3_1")
+        two_and_one(1, "codes_21_1")
+        quantised_b = quantise(late[0][:].rearrange("p c t -> p (c t)"), QUARTER, "3_b", "codes_3_b")
         sums_a = keep.tile([N, HALF], F32, name="sums_a", tag="sums_a", align_bytes=64)
         multiply([0, 1, 2, 3], quantised_a, (3,), False, sums_a)
         late.append(late_quarter(1, "codes_3_a"))
@@ -175,7 +175,7 @@ def tile_routed_moe_kernel(tc, xT, w_words, w_scales, gate, offs, out):
             )
 
         scatter(sums_a, 0, HALF)
-        quantised_c = quantise(late[1][:].rearrange("p c t -> p (c t)"), QUARTER, "3_c", "sums_a")
+        quantised_c = quantise(late[1][:].rearrange("p c t -> p (c t)"), QUARTER, "3_c", "codes_3_c")
         sums_c = keep.tile([N, QUARTER], F32, name="sums_c")
         multiply([6, 7], quantised_c, (3,), False, sums_c)
         scatter(sums_b, HALF, QUARTER)

@@ -35,7 +35,7 @@ def tile_routed_moe_kernel(tc, xT, w_words, w_scales, gate, offs, out):
         nc.vector.memset(w_planes[:].rearrange("p g n -> p (g n)").bitcast(I32), 0)
 
         x_view = xT.rearrange("(g p t) n -> g p t n", p=P, t=PACK)
-        place = {(2, 3): 0, (2, 2): 1, (2, 0): 2, (2, 1): 3, (0, 3): 4, (0, 2): 5, (0, 1): 6, (0, 0): 7}
+        place = {(2, 3): 0, (2, 2): 1, (2, 1): 2, (2, 0): 3, (0, 3): 4, (0, 2): 5, (0, 1): 6, (0, 0): 7}
         raw02 = keep.tile([P, 2 * PACK, T], F32, name="raw02", tag="raw02", align_bytes=64)
         raw1 = keep.tile([P, PACK, T], F32, name="raw1", tag="raw1", align_bytes=64)
         raw3 = [keep.tile([P, 2, T], F32, name="raw3_%d" % i, tag="raw3_%d" % i, align_bytes=64) for i in range(2)]
@@ -51,8 +51,7 @@ def tile_routed_moe_kernel(tc, xT, w_words, w_scales, gate, offs, out):
 
         for g, t in ((0, 0), (1, 0), (0, 1), (1, 1), (0, 2), (1, 2), (0, 3), (1, 3)):
             nc.sync.dma_start(plane(g, t), x_view[g, :, t, :])
-        nc.sync.dma_start(raw02[:, place[(2, 0)] : place[(2, 0)] + 2, :], x_view[2, :, 0:2, :])
-        for g, t in ((3, 0), (2, 2), (3, 1), (3, 2), (3, 3), (2, 3)):
+        for g, t in ((2, 0), (2, 1), (3, 0), (2, 2), (3, 1), (3, 2), (3, 3), (2, 3)):
             nc.sync.dma_start(plane(g, t), x_view[g, :, t, :])
         s_view = w_scales.rearrange("e a (q i) n -> i q (e a) n", i=4)
         for i in range(4):

@@ -135,8 +135,8 @@ def tile_routed_moe_kernel(tc, xT, w_words, w_scales, gate, offs, out):
         for t in range(PACK):
             gather_plane(2, t, True)
         middle = keep.tile([P, 2, 2, HALF, PACK], BF16, name="middle", tag="raw3_1", align_bytes=64)
-        for h in range(2):
-            merge(middle[:, h, 1, :, :], half(pairs[1], h), nc.gpsimd.tensor_copy)
+        merge(middle[:, 0, 1, :, :], half(pairs[1], 0), nc.gpsimd.tensor_copy)
+        merge(middle[:, 1, 1, :, :], half(pairs[1], 1), nc.scalar.copy)
         nc.vector.tensor_copy(
             middle[:, :, 0, :, :].bitcast(F32), pairs[2][:].bitcast(F32).rearrange("p u (h c) o -> p h c (u o)", h=2)
         )

@@ -51,7 +51,7 @@ def tile_routed_moe_kernel(tc, xT, w_words, w_scales, gate, offs, out):
 
         for g, t in ((0, 0), (1, 0), (0, 1), (1, 1), (0, 2), (1, 2), (0, 3), (1, 3)):
             nc.sync.dma_start(plane(g, t), x_view[g, :, t, :])
-        for g, t in ((2, 0), (2, 1), (3, 0), (2, 2), (3, 1), (3, 2), (3, 3), (2, 3)):
+        for g, t in ((2, 0), (2, 1), (3, 0), (2, 2), (3, 1), (3, 2), (2, 3), (3, 3)):
             nc.sync.dma_start(plane(g, t), x_view[g, :, t, :])
         s_view = w_scales.rearrange("e a (q i) n -> i q (e a) n", i=4)
         for i in range(4):

@@ -51,7 +51,7 @@ def tile_routed_moe_kernel(tc, xT, w_words, w_scales, gate, offs, out):
 
         for g, t in ((0, 0), (1, 0), (0, 1), (1, 1), (0, 2), (1, 2), (0, 3), (1, 3)):
             nc.sync.dma_start(plane(g, t), x_view[g, :, t, :])
-        for g, t in ((2, 0), (2, 1), (3, 0), (2, 2), (3, 1), (3, 2), (2, 3), (3, 3)):
+        for g, t in ((2, 0), (3, 0), (2, 1), (3, 1), (2, 2), (3, 2), (2, 3), (3, 3)):
             nc.sync.dma_start(plane(g, t), x_view[g, :, t, :])
         s_view = w_scales.rearrange("e a (q i) n -> i q (e a) n", i=4)
         for i in range(4):
@@ -126,10 +126,10 @@ def tile_routed_moe_kernel(tc, xT, w_words, w_scales, gate, offs, out):
             for h in range(2):
                 scalar_gather(half(pairs[1], h)[:, t // 2, :, t % 2], 1, t, h)
         first = keep.tile([P, 2, HALF, PACK], BF16, name="first", tag="raw1", align_bytes=64)
-        for h in range(2):
-            merge(first[:, h, :, :], half(pairs[0], h), nc.gpsimd.tensor_copy)
+        merge(first[:, 0, :, :], half(pairs[0], 0), nc.gpsimd.tensor_copy)
         for t in range(PACK):
             nc.gpsimd.tensor_copy(rounded[3][:, t, :], plane(3, t))
+        merge(first[:, 1, :, :], half(pairs[0], 1), nc.gpsimd.tensor_copy)
         for t in range(PACK):
             scalar_gather(last[0][:, :, t], 3, t, 0)
         for t in range(PACK):

@@ -122,7 +122,11 @@ def tile_routed_moe_kernel(tc, xT, w_words, w_scales, gate, offs, out):
 
         for t in range(PACK):
             gather_plane(0, t, t in (1, 2))
-            nc.gpsimd.tensor_copy(rounded[1][:, t, :], plane(1, t))
+            if t == 0:
+                nc.gpsimd.tensor_copy(rounded[1][:, t, 0:HALF], plane(1, t)[:, 0:HALF])
+                nc.scalar.copy(rounded[1][:, t, HALF:T], plane(1, t)[:, HALF:T])
+            else:
+                nc.gpsimd.tensor_copy(rounded[1][:, t, :], plane(1, t))
             for h in range(2):
                 scalar_gather(half(pairs[1], h)[:, t // 2, :, t % 2], 1, t, h)
         first = keep.tile([P, 2, HALF, PACK], BF16, name="first", tag="raw1", align_bytes=64)
@@ -137,9 +141,6 @@ def tile_routed_moe_kernel(tc, xT, w_words, w_scales, gate, offs, out):
         middle = keep.tile([P, 2, 2, HALF, PACK], BF16, name="middle", tag="raw3_1", align_bytes=64)
         merge(middle[:, 0, 1, :, :], half(pairs[1], 0), nc.gpsimd.tensor_copy)
         merge(middle[:, 1, 1, :, :], half(pairs[1], 1), nc.scalar.copy)
-        nc.vector.tensor_copy(
-            middle[:, :, 0, :, :].bitcast(F32), pairs[2][:].bitcast(F32).rearrange("p u (h c) o -> p h c (u o)", h=2)
-        )
         QUARTER = HALF // 2
 
         def quarter_of_list(q):
@@ -157,13 +158,20 @@ def tile_routed_moe_kernel(tc, xT, w_words, w_scales, gate, offs, out):
             multiply(experts_of(h), quantise(middle[:, h, :, :, :].rearrange("p a c t -> p (a c t)"), 2 * HALF, "21_%d" % h, tag), (2, 1), False)
 
         late = [late_quarter(0, "raw3_0")]
-        multiply(list(range(E)), quantise(first[:].rearrange("p h c t -> p (h c t)"), SLOTS, "0", "raw02"), (0,), True)
+
+        def zero(h):
+            multiply(experts_of(h), quantise(first[:, h, :, :].rearrange("p c t -> p (c t)"), HALF, "0_%d" % h, "raw02"), (0,), True)
+
+        merge(middle[:, 0, 0, :, :], half(pairs[2], 0), nc.vector.tensor_copy)
+        zero(0)
         two_and_one(0, "codes_21_0")
         quantised_a = quantise(last[0][:].rearrange("p c t -> p (c t)"), HALF, "3_a", "codes_3_a")
-        two_and_one(1, "codes_21_1")
-        quantised_b = quantise(late[0][:].rearrange("p c t -> p (c t)"), QUARTER, "3_b", "codes_3_b")
         sums_a = keep.tile([N, HALF], F32, name="sums_a", tag="sums_a", align_bytes=64)
         multiply([0, 1, 2, 3], quantised_a, (3,), False, sums_a)
+        merge(middle[:, 1, 0, :, :], half(pairs[2], 1), nc.vector.tensor_copy)
+        zero(1)
+        two_and_one(1, "codes_21_1")
+        quantised_b = quantise(late[0][:].rearrange("p c t -> p (c t)"), QUARTER, "3_b", "codes_3_b")
         late.append(late_quarter(1, "codes_3_a"))
         sums_b = keep.tile([N, QUARTER], F32, name="sums_b")
         multiply([4, 5], quantised_b, (3,), False, sums_b)

from contextlib import ExitStack

import concourse.mybir as mybir

K, T, E, C, N = 2048, 1024, 8, 128, 128
FLOPS = 2 * K * N * E * C

F32 = mybir.dt.float32
BF16 = mybir.dt.bfloat16
U32 = mybir.dt.uint32
I32 = mybir.dt.int32
U16 = mybir.dt.uint16
U8 = mybir.dt.uint8
FP8X4 = mybir.dt.float8_e4m3fn_x4
MULT = mybir.AluOpType.mult
COPY = mybir.ActivationFunctionType.Copy

P = 128
PACK = 4
PASSES = K // (P * PACK)
SLOTS = E * C
HALF = 512


def tile_routed_moe_kernel(tc, xT, w_words, w_scales, gate, offs, out):
    nc = tc.nc
    with ExitStack() as ctx:
        keep = ctx.enter_context(tc.tile_pool(name="keep", bufs=1))
        psum = ctx.enter_context(tc.psum_pool(name="psum", bufs=1))

        offsets = keep.tile([P, SLOTS // 16], U16, name="offsets")
        nc.sync.dma_start(offsets[:], offs)

        w_planes = keep.tile([P, E * PASSES, N], U8, name="w_planes", align_bytes=64)
        nc.vector.memset(w_planes[:].rearrange("p g n -> p (g n)").bitcast(I32), 0)

        x_view = xT.rearrange("(g p t) n -> g p t n", p=P, t=PACK)
        place = {(2, 3): 0, (2, 2): 1, (2, 1): 2, (2, 0): 3, (0, 3): 4, (0, 2): 5, (0, 1): 6, (0, 0): 7}
        raw02 = keep.tile([P, 2 * PACK, T], F32, name="raw02", tag="raw02", align_bytes=64)
        raw1 = keep.tile([P, PACK, T], F32, name="raw1", tag="raw1", align_bytes=64)
        raw3 = [keep.tile([P, 2, T], F32, name="raw3_%d" % i, tag="raw3_%d" % i, align_bytes=64) for i in range(2)]

        def plane(g, t):
            if g == 1:
                return raw1[:, t, :]
            if g == 3:
                return raw3[(0, 1, 1, 0)[t]][:, (0, 0, 1, 1)[t], :]
            return raw02[:, place[(g, t)], :]

        rounded = {g: keep.tile([P, PACK, T], BF16, name="rounded%d" % g) for g in (1, 3)}

        for g, t in ((0, 0), (1, 0), (0, 1), (1, 1), (0, 2), (1, 2), (0, 3), (1, 3)):
            nc.sync.dma_start(plane(g, t), x_view[g, :, t, :])
        for g, t in ((2, 0), (3, 0), (2, 1), (3, 1), (2, 2), (3, 2), (2, 3), (3, 3)):
            nc.sync.dma_start(plane(g, t), x_view[g, :, t, :])
        s_view = w_scales.rearrange("e a (q i) n -> i q (e a) n", i=4)
        for i in range(4):
            nc.sync.dma_start(w_planes[i:P:32, :, :].bitcast(I32), s_view[i].bitcast(I32))
        w_codes = [keep.tile([P, E, N], U32, name="w_codes%d" % a, align_bytes=64) for a in range(PASSES)]
        gate_sb = keep.tile([P, SLOTS], F32, name="gate_sb")
        for h in range(2):
            first_e = h * (HALF // C)
            for a in (0, 2, 1, 3):
                nc.sync.dma_start(
                    w_codes[a][:, first_e : first_e + HALF // C, :].bitcast(I32),
                    w_words[first_e : first_e + HALF // C, a].rearrange("e p n r -> p e (n r)").bitcast(I32),
                )
            if h == 0:
                nc.sync.dma_start(gate_sb[:], gate)

        acc = [psum.tile([N, C], F32, name="acc%d" % e) for e in range(E)]
        window = keep.tile([N, T], F32, name="window")

        pairs = {g: keep.tile([P, 2, SLOTS, 2], BF16, name="pairs%d" % g, tag="pairs%d" % g, align_bytes=64) for g in (0, 1, 2)}
        last = [keep.tile([P, HALF, PACK], BF16, name="last0", tag="last0", align_bytes=64)]

        def half_of_list(h):
            return offsets[:, h * (HALF // 16) : (h + 1) * (HALF // 16)]

        def half(tile4, h):
            return tile4[:, :, h * HALF : (h + 1) * HALF, :]

        def gather_plane(g, t, whole):
            if whole:
                two = raw02[:, place[(g, t)] : place[(g, t)] + 2, :].rearrange("p a n -> p (a n)")
                nc.vector.tensor_copy(pairs[g][:, t // 2, :, t % 2], two.indirect(offsets[:]))
            else:
                for h in range(2):
                    nc.vector.tensor_copy(half(pairs[g], h)[:, t // 2, :, t % 2], plane(g, t).indirect(half_of_list(h)))

        def merge(dst, src, copy):
            copy(dst.bitcast(F32), src.bitcast(F32).rearrange("p u c o -> p c (u o)"))

        def scalar_gather(dst, g, t, h):
            nc.scalar.activation(dst, rounded[g][:, t, :].indirect(half_of_list(h)), COPY)

        def quantise(values, slots, label, tag):
            codes = keep.tile([P, slots], U32, name="codes_" + label, tag=tag, align_bytes=64)
            scales = keep.tile([P, slots], U8, name="scales_" + label, align_bytes=64)
            nc.vector.quantize_mx(out=codes[:].bitcast(FP8X4), scales=scales[:], in_=values)
            return codes, scales

        def multiply(experts, quantised, passes, opens, sums=None):
            codes, scales = quantised
            for j, e in enumerate(experts):
                for a, g in enumerate(passes):
                    cols = slice((a * len(experts) + j) * C, (a * len(experts) + j + 1) * C)
                    nc.tensor.matmul_mx(
                        out=acc[e][:],
                        lhsT=w_codes[g][:, e, :].bitcast(FP8X4),
                        lhsT_scale=w_planes[:, e * PASSES + g, :],
                        rhs=codes[:, cols].bitcast(FP8X4),
                        rhs_scale=scales[:, cols],
                        start=opens,
                        stop=sums is not None,
                    )
                if sums is not None:
                    nc.scalar.copy(sums[:, j * C : (j + 1) * C], acc[e][:])

        def experts_of(h):
            return list(range(h * (HALF // C), (h + 1) * (HALF // C)))

        for t in range(PACK):
            gather_plane(0, t, t in (1, 2))
            if t == 0:
                nc.gpsimd.tensor_copy(rounded[1][:, t, 0:HALF], plane(1, t)[:, 0:HALF])
                nc.scalar.copy(rounded[1][:, t, HALF:T], plane(1, t)[:, HALF:T])
            else:
                nc.gpsimd.tensor_copy(rounded[1][:, t, :], plane(1, t))
            for h in range(2):
                scalar_gather(half(pairs[1], h)[:, t // 2, :, t % 2], 1, t, h)
        first = keep.tile([P, 2, HALF, PACK], BF16, name="first", tag="raw1", align_bytes=64)
        merge(first[:, 0, :, :], half(pairs[0], 0), nc.gpsimd.tensor_copy)
        for t in range(PACK):
            nc.gpsimd.tensor_copy(rounded[3][:, t, :], plane(3, t))
        merge(first[:, 1, :, :], half(pairs[0], 1), nc.gpsimd.tensor_copy)
        for t in range(PACK):
            scalar_gather(last[0][:, :, t], 3, t, 0)
        for t in range(PACK):
            gather_plane(2, t, True)
        middle = keep.tile([P, 2, 2, HALF, PACK], BF16, name="middle", tag="raw3_1", align_bytes=64)
        merge(middle[:, 0, 1, :, :], half(pairs[1], 0), nc.gpsimd.tensor_copy)
        merge(middle[:, 1, 1, :, :], half(pairs[1], 1), nc.scalar.copy)
        QUARTER = HALF // 2

        def quarter_of_list(q):
            return offsets[:, (HALF + q * QUARTER) // 16 : (HALF + (q + 1) * QUARTER) // 16]

        def late_quarter(q, tag):
            pairs3 = keep.tile([P, 2, QUARTER, 2], BF16, name="pairs3_%d" % q, tag=tag, align_bytes=64)
            for t in range(PACK):
                nc.scalar.activation(pairs3[:, t // 2, :, t % 2], rounded[3][:, t, :].indirect(quarter_of_list(q)), COPY)
            values = keep.tile([P, QUARTER, PACK], BF16, name="late%d" % q, align_bytes=64)
            merge(values[:], pairs3[:], nc.scalar.copy)
            return values

        def two_and_one(h, tag):
            multiply(experts_of(h), quantise(middle[:, h, :, :, :].rearrange("p a c t -> p (a c t)"), 2 * HALF, "21_%d" % h, tag), (2, 1), False)

        late = [late_quarter(0, "raw3_0")]

        def zero(h):
            multiply(experts_of(h), quantise(first[:, h, :, :].rearrange("p c t -> p (c t)"), HALF, "0_%d" % h, "raw02"), (0,), True)

        merge(middle[:, 0, 0, :, :], half(pairs[2], 0), nc.vector.tensor_copy)
        zero(0)
        two_and_one(0, "codes_21_0")
        quantised_a = quantise(last[0][:].rearrange("p c t -> p (c t)"), HALF, "3_a", "codes_3_a")
        sums_a = keep.tile([N, HALF], F32, name="sums_a", tag="sums_a", align_bytes=64)
        multiply([0, 1, 2, 3], quantised_a, (3,), False, sums_a)
        merge(middle[:, 1, 0, :, :], half(pairs[2], 1), nc.vector.tensor_copy)
        zero(1)
        two_and_one(1, "codes_21_1")
        quantised_b = quantise(late[0][:].rearrange("p c t -> p (c t)"), QUARTER, "3_b", "codes_3_b")
        late.append(late_quarter(1, "codes_3_a"))
        sums_b = keep.tile([N, QUARTER], F32, name="sums_b")
        multiply([4, 5], quantised_b, (3,), False, sums_b)

        def scatter(values, first_slot, slots):
            nc.vector.tensor_tensor(
                window[:].indirect(offsets[:, first_slot // 16 : (first_slot + slots) // 16]), values[:], gate_sb[:, first_slot : first_slot + slots], MULT
            )

        scatter(sums_a, 0, HALF)
        quantised_c = quantise(late[1][:].rearrange("p c t -> p (c t)"), QUARTER, "3_c", "codes_3_c")
        sums_c = keep.tile([N, QUARTER], F32, name="sums_c")
        multiply([6, 7], quantised_c, (3,), False, sums_c)
        scatter(sums_b, HALF, QUARTER)
        scatter(sums_c, HALF + QUARTER, QUARTER)
        nc.sync.dma_start(out, window[:])
